import numpy as np
import ml_dtypes


def mxq(x, axis, fmt="e4m3"):
    dtype, down = {"e4m3": (ml_dtypes.float8_e4m3fn, 7), "e5m2": (ml_dtypes.float8_e5m2, 14)}[fmt]
    v = np.moveaxis(np.asarray(x, np.float32).astype(ml_dtypes.bfloat16).astype(np.float64), axis, -1)
    blocks = v.reshape(v.shape[:-1] + (-1, 32))
    amax = np.abs(blocks).max(-1, keepdims=True)
    byte = np.maximum(np.where(amax > 0, np.frexp(amax)[1] - 1 + 127, 0) - down, 1)
    scale = np.exp2(byte - 127.0)
    codes = (blocks / scale).astype(np.float32).astype(dtype).astype(np.float64)
    return np.moveaxis((codes * scale).reshape(v.shape), -1, axis)


WIDE = False


def mx_kscale(k):
    if not WIDE:
        return np.ones(k)
    levels = np.array([10, -10, 5, -5, 0])
    if k % 512:
        return np.exp2(np.random.permutation(np.resize(levels, k // 32))).repeat(32)
    a = np.empty((k // 512, 16))
    for p in range(k // 512):
        a[p, :8] = np.random.permutation(np.resize(levels, 8))
        for g in range(8):
            far = levels[np.abs(levels - a[p, g]) >= 10]
            a[p, g + 8] = far[np.random.randint(len(far))]
    return np.exp2(a.ravel()).repeat(32)


BF16 = ml_dtypes.bfloat16


def bf(x):
    return np.asarray(x, np.float32).astype(BF16)


def f64(x):
    return np.asarray(x).astype(np.float64)


E2M1 = np.array([0.0, 0.5, 1.0, 1.5, 2.0, 3.0, 4.0, 6.0, -0.0, -0.5, -1.0, -1.5, -2.0, -3.0, -4.0, -6.0])


def pack_weight(w, fmt):
    k, n = w.shape
    w = f64(bf(w)).reshape(k // 32, 32, n)
    amax = np.abs(w).max(1)
    if fmt == "e4m3":
        byte = np.frexp(amax)[1] - 1 + 127 - 7
    else:
        mant, ex = np.frexp(amax / 6.0)
        byte = np.where(mant > 0.5, ex, ex - 1) + 127
    byte = np.clip(np.where(amax > 0, byte, 1), 1, 254)
    scaled = (w * np.exp2(127.0 - byte)[:, None, :]).reshape(k, n).astype(np.float32)
    by_word = np.ascontiguousarray(scaled.reshape(k // 512, 128, 4, n).transpose(0, 1, 3, 2))
    if fmt == "e4m3":
        words = by_word.astype(ml_dtypes.float8_e4m3fn).view(np.uint8)
    else:
        c = by_word.astype(ml_dtypes.float4_e2m1fn).view(np.uint8) & 0xF
        words = c[..., 0::2] | (c[..., 1::2] << 4)
    return np.ascontiguousarray(words), np.ascontiguousarray(byte.astype(np.uint8).reshape(k // 512, 16, n))


def unpack_weight(words, scales, fmt):
    g, p, n, _ = words.shape
    if fmt == "e4m3":
        vals = np.ascontiguousarray(words).view(ml_dtypes.float8_e4m3fn).astype(np.float64)
    else:
        nib = np.empty((g, p, n, 4), np.uint8)
        nib[..., 0::2] = words & 0xF
        nib[..., 1::2] = words >> 4
        vals = E2M1[nib]
    vals = vals * np.repeat(np.exp2(scales.astype(np.float64) - 127.0), 8, axis=1)[..., None]
    return vals.transpose(0, 1, 3, 2).reshape(g * 512, n)
def pack4(w):
    words, scales = pack_weight(w, "e2m1")
    return words.reshape(words.shape[0], 128, -1), scales


def unpack4(words, scales):
    return unpack_weight(words.reshape(words.shape[0], 128, -1, 2), scales, "e2m1")


def planes(Y):
    n, m = Y.shape
    b = f64(bf(Y)).reshape(n // 32, 32, m)
    amax = np.abs(b).max(1)
    byte = np.clip(np.where(amax > 0, np.frexp(amax)[1] - 1 + 127 - 7, 1), 1, 254)
    codes = (b * np.exp2(127.0 - byte)[:, None, :]).reshape(n, m).astype(np.float32).astype(ml_dtypes.float8_e4m3fn).view(np.uint8)
    words = codes.reshape(n // 512, 128, 4, m).transpose(0, 1, 3, 2)
    return np.ascontiguousarray(words), np.ascontiguousarray(byte.astype(np.uint8).reshape(n // 512, 16, m))


T, D, F = 512, 1024, 4096

GELU_A = 0.7978845608028654
GELU_B = 0.044715

def setup_inputs():
    s = mx_kscale(D)
    t = mx_kscale(F)
    size = np.exp(0.8 * np.random.randn(D))
    states = bf(np.random.randn(T, D) * size)
    in_scale = bf((1 + 0.1 * np.random.randn(D)) / size * s)
    w1_words, w1_scales = pack4(np.random.randn(D, F) / np.sqrt(D) / s[:, None])
    b1 = bf(0.3 * np.random.randn(F))
    mid_scale = bf(np.exp(0.3 * np.random.randn(F)) * t)
    w2_words, w2_scales = pack4(np.random.randn(F, D) / np.sqrt(F) * size / t[:, None])
    b2 = bf(0.3 * np.random.randn(D) * size)
    return {"states": states, "in_scale": in_scale, "w1_words": w1_words, "w1_scales": w1_scales,
            "b1": b1, "mid_scale": mid_scale, "w2_words": w2_words, "w2_scales": w2_scales, "b2": b2}

def reference(states, in_scale, w1_words, w1_scales, b1, mid_scale, w2_words, w2_scales, b2):
    r = f64(states)
    W1 = unpack4(w1_words, w1_scales)
    W2 = unpack4(w2_words, w2_scales)
    x = r * f64(in_scale)
    z = (mxq(x, 1, "e4m3") @ W1) + f64(b1)
    h = 0.5 * z * (1 + np.tanh(GELU_A * (z + GELU_B * z * z * z))) * f64(mid_scale)
    y = (mxq(h, 1, "e4m3") @ W2) + f64(b2) + r
    Y = y.T
    words, scales = planes(Y)
    return y, words, scales

@@ -1,0 +1,377 @@
+from contextlib import ExitStack
+
+import concourse.mybir as mybir
+from concourse.masks import make_identity
+
+T, D, F = 512, 1024, 4096
+FLOPS = 2 * 2 * T * D * F
+
+F32 = mybir.dt.float32
+BF16 = mybir.dt.bfloat16
+I32 = mybir.dt.int32
+U32 = mybir.dt.uint32
+U8 = mybir.dt.uint8
+FP8X4 = mybir.dt.float8_e4m3fn_x4
+FP4X4 = mybir.dt.float4_e2m1fn_x4
+ALU = mybir.AluOpType
+ACT = mybir.ActivationFunctionType
+
+P = 128
+PACK = 4
+KP = P * PACK
+DG = D // KP
+FG = F // KP
+TT = T // P
+LAG = 3
+SHARE = 256
+EARLY = 3
+
+
+def tile_gelu_feedforward_residual_head_h1_kernel(
+    tc, states, in_scale, w1_words, w1_scales, b1, mid_scale, w2_words, w2_scales, b2, out_0, out_1, out_2
+):
+    nc = tc.nc
+    with ExitStack() as ctx:
+        keep = ctx.enter_context(tc.tile_pool(name="keep", bufs=1))
+        work = ctx.enter_context(tc.tile_pool(name="work", bufs=2))
+        psum = ctx.enter_context(tc.psum_pool(name="psum", bufs=1))
+        ctx.enter_context(tc.manual_schedule())
+
+        def kept(name, shape, dtype):
+            return keep.tile(shape, dtype, name=name, tag=name, align_bytes=64)
+
+        def bank(index):
+            return psum.tile([P, KP], F32, name="bank%d" % index, tag="bank%d" % index)
+
+        ident = kept("ident", [P, P], F32)
+        make_identity(nc, ident[:])
+        vec = kept("vec", [P, KP], BF16)
+        nc.vector.memset(vec[:].bitcast(I32), 0)
+        warm = kept("warm", [P, 2], F32)
+        nc.vector.memset(warm[:, 0:1], 0.0)
+        nc.scalar.activation(out=warm[:, 1:2], in_=warm[:, 0:1], func=ACT.Gelu_apprx_tanh)
+        plane1 = kept("plane1", [P, FG, DG * KP], U8)
+        nc.vector.memset(plane1[:].rearrange("p c n -> p (c n)").bitcast(I32), 0)
+        plane2 = kept("plane2", [P, FG, D], U8)
+        nc.gpsimd.memset(plane2[:].rearrange("p c n -> p (c n)").bitcast(I32), 0)
+
+        s1_raw = kept("s1_raw", [P, DG, KP], U8)
+        nc.sync.dma_start(
+            out=s1_raw[:].bitcast(I32),
+            in_=w1_scales.rearrange("g q (c n) -> (q c) g n", c=FG).bitcast(I32),
+        )
+
+        st = []
+
+        def load_states(g):
+            tile = kept("st%d" % g, [P, TT, KP], BF16)
+            nc.sync.dma_start(out=tile[:], in_=states[:, g * KP : (g + 1) * KP].rearrange("(j p) n -> p j n", p=P))
+            st.append(tile)
+
+        w1_raw = []
+
+        def load_w1(c):
+            tile = kept("w1_raw%d" % c, [P, DG, 2 * KP], U8)
+            src = w1_words[:, :, 2 * KP * c : 2 * KP * (c + 1)].rearrange("g p n -> p g n")
+            nc.sync.dma_start(out=tile[:].bitcast(I32), in_=src.bitcast(I32))
+            w1_raw.append(tile)
+
+        w2 = []
+
+        def load_w2(pair):
+            tile = kept("w2_%d" % pair, [P, 2, 2 * D], U8)
+            src = w2_words[2 * pair : 2 * pair + 2].rearrange("g p n -> p g n")
+            nc.sync.dma_start(out=tile[:].bitcast(I32), in_=src.bitcast(I32))
+            w2.append(tile)
+
+        load_states(0)
+        nc.sync.dma_start(out=vec[2 * FG : 2 * FG + DG, :], in_=in_scale.rearrange("(g n) -> g n", n=KP))
+        nc.sync.dma_start(out=vec[0:FG, :], in_=b1.rearrange("(g n) -> g n", n=KP))
+        nc.sync.dma_start(out=vec[FG : 2 * FG, :], in_=mid_scale.rearrange("(g n) -> g n", n=KP))
+        load_w1(0)
+        load_states(1)
+        load_w1(1)
+
+        s1_sorted = kept("s1_sorted", [P, DG * KP], U8)
+        nc.vector.tensor_copy(
+            out=s1_sorted[:].rearrange("p (g t m) -> p g t m", g=DG, t=PACK),
+            in_=s1_raw[:].rearrange("p g (m t) -> p g t m", t=PACK),
+        )
+        for q in range(4):
+            nc.sync.dma_start(
+                out=plane1[32 * q : 32 * q + 4, :, :].bitcast(I32),
+                in_=s1_sorted[32 * q : 32 * q + 32, :].bitcast(I32),
+            )
+        for q in range(4):
+            nc.sync.dma_start(
+                out=plane2[32 * q : 32 * q + 4, :, :].bitcast(I32),
+                in_=w2_scales[:, 4 * q : 4 * q + 4, :].rearrange("g r n -> r g n").bitcast(I32),
+            )
+        load_w1(2)
+        load_w2(0)
+        load_w1(3)
+        load_w1(4)
+        load_w2(1)
+        load_w1(5)
+        load_w1(6)
+        load_w2(2)
+        load_w1(7)
+        load_w2(3)
+        b2_rows = kept("b2_rows", [P, D], BF16)
+        nc.sync.dma_start(out=b2_rows[:], in_=b2.partition_broadcast(P))
+
+        def word_transposes(dst, src_words):
+            for u in range(2):
+                nc.tensor.transpose(dst[u], src_words[:, u::2], ident[:])
+
+        vec_t = bank(0)
+        word_transposes([vec_t[:, u * P : (u + 1) * P] for u in range(2)], vec[:].bitcast(F32))
+        vec_view = vec_t[:, 0 : 2 * P].bitcast(BF16).rearrange("p (u r e) -> p r u e", u=2, e=2)
+        x_gain = kept("x_gain", [P, DG, PACK], BF16)
+        nc.scalar.copy(out=x_gain[:].rearrange("p r (u e) -> p r u e", e=2), in_=vec_view[:, 2 * FG : 2 * FG + DG])
+        chan = kept("chan", [P, 2 * FG, PACK], F32)
+        nc.scalar.copy(out=chan[:].rearrange("p r (u e) -> p r u e", e=2), in_=vec_view[:, 0 : 2 * FG])
+
+        w1 = []
+
+        def sort_w1(c):
+            tile = kept("w1_%d" % c, [P, DG, PACK, 2 * P], U8)
+            nc.vector.tensor_copy(
+                out=tile[:].rearrange("p g t (m b) -> p g t m b", b=2),
+                in_=w1_raw[c][:].rearrange("p g (m t b) -> p g t m b", t=PACK, b=2),
+            )
+            w1.append(tile)
+
+        sort_w1(0)
+
+        x_grouped = [kept("x_grouped%d" % g, [P, T * PACK], BF16) for g in range(DG)]
+        x_codes = [kept("x_codes%d" % g, [P, T], U32) for g in range(DG)]
+        x_scales = [kept("x_scales%d" % g, [P, T], U8) for g in range(DG)]
+
+        def x_half(g, half):
+            acc = bank(2 + 2 * g + half)
+            for jj in range(2):
+                words = st[g][:, 2 * half + jj, :].bitcast(F32)
+                word_transposes([acc[:, (2 * u + jj) * P : (2 * u + jj + 1) * P] for u in range(2)], words)
+            nc.vector.tensor_tensor(
+                out=x_grouped[g][:, half * 1024 : (half + 1) * 1024].rearrange("p (r u e) -> p r u e", u=2, e=2),
+                in0=acc[:].bitcast(BF16).rearrange("p (u r e) -> p r u e", u=2, e=2),
+                in1=x_gain[:, g : g + 1, :].rearrange("p o (u e) -> p o u e", e=2).to_broadcast([P, 2 * P, 2, 2]),
+                op=ALU.mult,
+            )
+
+        def quantize_x(g):
+            nc.vector.quantize_mx(out=x_codes[g][:].bitcast(FP8X4), scales=x_scales[g][:], in_=x_grouped[g][:])
+
+        x_half(0, 0)
+        x_half(0, 1)
+        x_half(1, 0)
+        quantize_x(0)
+        x_half(1, 1)
+        sort_w1(1)
+        quantize_x(1)
+        sort_w1(2)
+
+        def up_pass(acc, c, t, g):
+            nc.tensor.matmul_mx(
+                out=acc[:],
+                lhsT=w1[c][:, g, t, :].bitcast(FP4X4),
+                lhsT_scale=plane1[:, c, g * KP + t * P : g * KP + (t + 1) * P],
+                rhs=x_codes[g][:].bitcast(FP8X4),
+                rhs_scale=x_scales[g][:],
+                start=(g == 0),
+                stop=(g == DG - 1),
+            )
+
+        h_codes = [kept("h_codes%d" % c, [P, T], U32) for c in range(FG)]
+        h_scales = [kept("h_scales%d" % c, [P, T], U8) for c in range(FG)]
+        y_acc = {}
+
+        def down_pass(c, j, h):
+            if c == 0:
+                y_acc[j, h] = bank((2 + 2 * j + h) % 8)
+            nc.tensor.matmul_mx(
+                out=y_acc[j, h][:],
+                lhsT=h_codes[c][:, j * P : (j + 1) * P].bitcast(FP8X4),
+                lhsT_scale=h_scales[c][:, j * P : (j + 1) * P],
+                rhs=w2[c // 2][:, c % 2, 2 * KP * h : 2 * KP * (h + 1)].bitcast(FP4X4),
+                rhs_scale=plane2[:, c, KP * h : KP * (h + 1)],
+                start=(c == 0),
+                stop=(c == FG - 1),
+            )
+
+        gelu = {}
+        shared = {}
+        h_grouped = {}
+
+        def share_of(c):
+            return SHARE if c >= LAG else 0
+
+        def gelu_out(c, t, acc):
+            if t == 0:
+                gelu[c] = work.tile([P, PACK, T], F32, name="gelu", tag="gelu", bufs=4, align_bytes=64)
+            nc.scalar.activation(out=gelu[c][:, t, :], in_=acc[:], func=ACT.Gelu_apprx_tanh, bias=chan[:, c, t : t + 1])
+
+        def scalar_gain(c, t):
+            n = share_of(c)
+            if n == 0:
+                return
+            if t == 0:
+                shared[c] = work.tile([P, PACK, SHARE], BF16, name="shared", tag="shared", bufs=2, align_bytes=64)
+            nc.scalar.activation(
+                out=shared[c][:, t, :], in_=gelu[c][:, t, 0:n], func=ACT.Copy, scale=chan[:, FG + c, t : t + 1]
+            )
+
+        def vector_gain(c):
+            n = share_of(c)
+            h_grouped[c] = work.tile([P, T, PACK], BF16, name="h_grouped", tag="h_grouped", bufs=2, align_bytes=64)
+            runs = (T - n) // 4
+            nc.vector.tensor_tensor(
+                out=h_grouped[c][:, n:T, :].rearrange("p (a i) t -> p a t i", i=4),
+                in0=gelu[c][:, :, n:T].rearrange("p t (a i) -> p a t i", i=4),
+                in1=chan[:, FG + c : FG + c + 1, :].unsqueeze(3).to_broadcast([P, runs, PACK, 4]),
+                op=ALU.mult,
+            )
+
+        def interleave_shared(c):
+            n = share_of(c)
+            if n == 0:
+                return
+            nc.vector.tensor_copy(
+                out=h_grouped[c][:, 0:n, :].rearrange("p (a i) t -> p a t i", i=4),
+                in_=shared[c][:].rearrange("p t (a i) -> p a t i", i=4),
+            )
+
+        def quantize_h(c):
+            nc.vector.quantize_mx(
+                out=h_codes[c][:].bitcast(FP8X4),
+                scales=h_scales[c][:],
+                in_=h_grouped[c][:].rearrange("p m t -> p (m t)"),
+            )
+
+        pieces = [(j, h) for j in range(TT) for h in range(DG)]
+        rb = {}
+
+        def residual_bias(j, h):
+            rb[j, h] = kept("rb%d_%d" % (j, h), [P, KP], F32)
+            nc.vector.tensor_tensor(
+                out=rb[j, h][:], in0=st[h][:, j, :], in1=b2_rows[:, h * KP : (h + 1) * KP], op=ALU.add
+            )
+
+        def vector_group(c):
+            vector_gain(c)
+            interleave_shared(c)
+            if c + LAG < FG:
+                sort_w1(c + LAG)
+            else:
+                first = 3 * (c + LAG - FG)
+                for piece in pieces[first : min(first + 3, 7)]:
+                    residual_bias(*piece)
+            quantize_h(c)
+
+        resident = pieces[:6]
+        for c in range(FG):
+            wide = c < LAG
+            ring = [0, 1, 6, 7] if wide else [0, 1]
+            down = [(c - LAG, j, h) for j, h in resident] if not wide else []
+            if c == 0:
+                accs = [bank(ring[t]) for t in range(PACK)]
+                for g in range(DG):
+                    for t in range(PACK):
+                        up_pass(accs[t], c, t, g)
+            for t in range(PACK):
+                if c == 0:
+                    acc = accs[t]
+                else:
+                    acc = bank(ring[t % len(ring)])
+                    for g in range(DG):
+                        up_pass(acc, c, t, g)
+                gelu_out(c, t, acc)
+                if t > 0:
+                    scalar_gain(c, t - 1)
+                elif c > 0:
+                    scalar_gain(c - 1, PACK - 1)
+                    vector_group(c - 1)
+                for item in down[(3 * t + 1) // 2 : (3 * t + 4) // 2]:
+                    down_pass(*item)
+        scalar_gain(FG - 1, PACK - 1)
+        vector_group(FG - 1)
+        residual_bias(*pieces[7])
+
+        for c in range(FG - LAG, FG - 1):
+            for j, h in resident:
+                down_pass(c, j, h)
+        late = [(c, j, h) for j, h in pieces[6:] for c in range(FG)]
+        for item in late[:EARLY]:
+            down_pass(*item)
+        for j, h in resident:
+            down_pass(FG - 1, j, h)
+        late = late[EARLY:]
+
+        y_codes = kept("y_codes", [P, DG, T], U32)
+        y_scales = kept("y_scales", [P, T], U8)
+        words_out = out_1.rearrange("g p m t -> p g (m t)").bitcast(I32)
+        y = {}
+        y_pairs = {}
+        y_t = {}
+        y_grouped = {}
+
+        def add_residual(j, h):
+            y[j, h] = kept("y%d_%d" % (j, h), [P, KP], F32)
+            nc.vector.tensor_tensor(out=y[j, h][:], in0=y_acc[j, h][:], in1=rb[j, h][:], op=ALU.add)
+            nc.sync.dma_start(out=out_0[j * P : (j + 1) * P, h * KP : (h + 1) * KP], in_=y[j, h][:])
+
+        def round_y(j, h):
+            y_pairs[j, h] = work.tile([P, KP], BF16, name="y_pairs", tag="y_pairs", bufs=4, align_bytes=64)
+            nc.scalar.copy(
+                out=y_pairs[j, h][:].rearrange("p (u m e) -> p u m e", u=2, e=2),
+                in_=y[j, h][:].rearrange("p (m u e) -> p u m e", u=2, e=2),
+            )
+
+        def turn_y(j, h):
+            y_t[j, h] = bank((2 + 2 * j + h) % 8)
+            words = y_pairs[j, h][:].bitcast(F32)
+            for u in range(2):
+                nc.tensor.transpose(y_t[j, h][:, u * P : (u + 1) * P], words[:, u * P : (u + 1) * P], ident[:])
+
+        def group_y(j, h):
+            y_grouped[j, h] = work.tile([P, KP], BF16, name="y_grouped", tag="y_grouped", bufs=4, align_bytes=64)
+            nc.scalar.copy(
+                out=y_grouped[j, h][:].bitcast(F32).rearrange("p (r u) -> p r u", u=2),
+                in_=y_t[j, h][:, 0 : 2 * P].rearrange("p (u r) -> p r u", u=2),
+            )
+
+        def quantize_y(j, h):
+            nc.vector.quantize_mx(
+                out=y_codes[:, h, j * P : (j + 1) * P].bitcast(FP8X4),
+                scales=y_scales[4 * h : P, j * P : (j + 1) * P],
+                in_=y_grouped[j, h][:],
+            )
+            if h == DG - 1:
+                nc.sync.dma_start(
+                    out=words_out[:, :, j * P : (j + 1) * P], in_=y_codes[:, :, j * P : (j + 1) * P].bitcast(I32)
+                )
+
+        steps = len(pieces)
+        for i in range(steps + 3):
+            if i < steps:
+                j, h = pieces[i]
+                add_residual(j, h)
+                round_y(j, h)
+            if i in (1, 3, 5):
+                count = 4 if i < 5 else len(late)
+                for item in late[:count]:
+                    down_pass(*item)
+                late = late[count:]
+            if 1 <= i <= steps and (i % 2 == 0 or i >= 7):
+                lo = i - 2 if i <= 6 else i - 1
+                for k in range(lo, i):
+                    turn_y(*pieces[k])
+                for k in range(lo, i):
+                    group_y(*pieces[k])
+            if i >= 3:
+                quantize_y(*pieces[i - 3])
+        for q in range(4):
+            nc.sync.dma_start(
+                out=out_2[:, 4 * q : 4 * q + 4, :].bitcast(I32), in_=y_scales[32 * q : 32 * q + 8, :].bitcast(I32)
+            )

@@ -23,8 +23,17 @@ DG = D // KP
 FG = F // KP
 TT = T // P
 LAG = 3
-SHARE = 256
-EARLY = 3
+SHARE = 320
+SHARE_FROM = 2
+SHARE_LAST = 256
+EARLY_A = 0
+EARLY_B = 2
+STEP = 6
+AHEAD = 4
+RB_RATE = 2
+XORD = 0
+RB_MORE = 0
+G0 = 2
 
 
 def tile_gelu_feedforward_residual_head_h1_kernel(
@@ -47,12 +56,16 @@ def tile_gelu_feedforward_residual_head_h1_kernel(
         make_identity(nc, ident[:])
         vec = kept("vec", [P, KP], BF16)
         nc.vector.memset(vec[:].bitcast(I32), 0)
+        nc.scalar.dma_start(out=vec[2 * FG : 2 * FG + DG, :], in_=in_scale.rearrange("(g n) -> g n", n=KP))
+        nc.scalar.dma_start(out=vec[0:FG, :], in_=b1.rearrange("(g n) -> g n", n=KP))
+        nc.scalar.dma_start(out=vec[FG : 2 * FG, :], in_=mid_scale.rearrange("(g n) -> g n", n=KP))
         warm = kept("warm", [P, 2], F32)
         nc.vector.memset(warm[:, 0:1], 0.0)
         nc.scalar.activation(out=warm[:, 1:2], in_=warm[:, 0:1], func=ACT.Gelu_apprx_tanh)
-        plane1 = kept("plane1", [P, FG, DG * KP], U8)
-        nc.vector.memset(plane1[:].rearrange("p c n -> p (c n)").bitcast(I32), 0)
+        plane1 = [kept("plane1_%d" % g, [P, FG, KP], U8) for g in range(DG)]
         plane2 = kept("plane2", [P, FG, D], U8)
+        for tile in plane1:
+            nc.vector.memset(tile[:].rearrange("p c n -> p (c n)").bitcast(I32), 0)
         nc.gpsimd.memset(plane2[:].rearrange("p c n -> p (c n)").bitcast(I32), 0)
 
         s1_raw = kept("s1_raw", [P, DG, KP], U8)
@@ -61,12 +74,25 @@ def tile_gelu_feedforward_residual_head_h1_kernel(
             in_=w1_scales.rearrange("g q (c n) -> (q c) g n", c=FG).bitcast(I32),
         )
 
-        st = []
+        def place_s1():
+            tile = kept("s1_sorted", [P, DG, KP], U8)
+            nc.vector.tensor_copy(
+                out=tile[:].rearrange("p g (t m) -> p g t m", t=PACK),
+                in_=s1_raw[:].rearrange("p g (m t) -> p g t m", t=PACK),
+            )
+            for g in range(DG):
+                for q in range(4):
+                    nc.sync.dma_start(
+                        out=plane1[g][32 * q : 32 * q + 4, :, :].bitcast(I32),
+                        in_=tile[32 * q : 32 * q + 32, g, :].bitcast(I32),
+                    )
 
-        def load_states(g):
-            tile = kept("st%d" % g, [P, TT, KP], BF16)
-            nc.sync.dma_start(out=tile[:], in_=states[:, g * KP : (g + 1) * KP].rearrange("(j p) n -> p j n", p=P))
-            st.append(tile)
+        st = {}
+
+        def load_states(g, half):
+            st[g, half] = kept("st%d_%d" % (g, half), [P, 2, KP], BF16)
+            src = states[half * 2 * P : (half + 1) * 2 * P, g * KP : (g + 1) * KP]
+            nc.sync.dma_start(out=st[g, half][:], in_=src.rearrange("(j p) n -> p j n", p=P))
 
         w1_raw = []
 
@@ -84,32 +110,20 @@ def tile_gelu_feedforward_residual_head_h1_kernel(
             nc.sync.dma_start(out=tile[:].bitcast(I32), in_=src.bitcast(I32))
             w2.append(tile)
 
-        load_states(0)
-        nc.sync.dma_start(out=vec[2 * FG : 2 * FG + DG, :], in_=in_scale.rearrange("(g n) -> g n", n=KP))
-        nc.sync.dma_start(out=vec[0:FG, :], in_=b1.rearrange("(g n) -> g n", n=KP))
-        nc.sync.dma_start(out=vec[FG : 2 * FG, :], in_=mid_scale.rearrange("(g n) -> g n", n=KP))
         load_w1(0)
-        load_states(1)
+        for g in range(DG):
+            for half in range(2):
+                load_states(g, half)
+        place_s1()
         load_w1(1)
-
-        s1_sorted = kept("s1_sorted", [P, DG * KP], U8)
-        nc.vector.tensor_copy(
-            out=s1_sorted[:].rearrange("p (g t m) -> p g t m", g=DG, t=PACK),
-            in_=s1_raw[:].rearrange("p g (m t) -> p g t m", t=PACK),
-        )
-        for q in range(4):
-            nc.sync.dma_start(
-                out=plane1[32 * q : 32 * q + 4, :, :].bitcast(I32),
-                in_=s1_sorted[32 * q : 32 * q + 32, :].bitcast(I32),
-            )
+        load_w1(2)
+        load_w1(3)
         for q in range(4):
             nc.sync.dma_start(
                 out=plane2[32 * q : 32 * q + 4, :, :].bitcast(I32),
                 in_=w2_scales[:, 4 * q : 4 * q + 4, :].rearrange("g r n -> r g n").bitcast(I32),
             )
-        load_w1(2)
         load_w2(0)
-        load_w1(3)
         load_w1(4)
         load_w2(1)
         load_w1(5)
@@ -151,7 +165,7 @@ def tile_gelu_feedforward_residual_head_h1_kernel(
         def x_half(g, half):
             acc = bank(2 + 2 * g + half)
             for jj in range(2):
-                words = st[g][:, 2 * half + jj, :].bitcast(F32)
+                words = st[g, half][:, jj, :].bitcast(F32)
                 word_transposes([acc[:, (2 * u + jj) * P : (2 * u + jj + 1) * P] for u in range(2)], words)
             nc.vector.tensor_tensor(
                 out=x_grouped[g][:, half * 1024 : (half + 1) * 1024].rearrange("p (r u e) -> p r u e", u=2, e=2),
@@ -165,18 +179,22 @@ def tile_gelu_feedforward_residual_head_h1_kernel(
 
         x_half(0, 0)
         x_half(0, 1)
-        x_half(1, 0)
-        quantize_x(0)
+        if XORD:
+            quantize_x(0)
+            x_half(1, 0)
+        else:
+            x_half(1, 0)
+            quantize_x(0)
         x_half(1, 1)
-        sort_w1(1)
         quantize_x(1)
-        sort_w1(2)
+        for c in range(1, AHEAD):
+            sort_w1(c)
 
         def up_pass(acc, c, t, g):
             nc.tensor.matmul_mx(
                 out=acc[:],
                 lhsT=w1[c][:, g, t, :].bitcast(FP4X4),
-                lhsT_scale=plane1[:, c, g * KP + t * P : g * KP + (t + 1) * P],
+                lhsT_scale=plane1[g][:, c, t * P : (t + 1) * P],
                 rhs=x_codes[g][:].bitcast(FP8X4),
                 rhs_scale=x_scales[g][:],
                 start=(g == 0),
@@ -205,7 +223,7 @@ def tile_gelu_feedforward_residual_head_h1_kernel(
         h_grouped = {}
 
         def share_of(c):
-            return SHARE if c >= LAG else 0
+            return SHARE_LAST if c == FG - 1 else SHARE if c >= SHARE_FROM else 0
 
         def gelu_out(c, t, acc):
             if t == 0:
@@ -217,19 +235,21 @@ def tile_gelu_feedforward_residual_head_h1_kernel(
             if n == 0:
                 return
             if t == 0:
-                shared[c] = work.tile([P, PACK, SHARE], BF16, name="shared", tag="shared", bufs=2, align_bytes=64)
+                shared[c] = work.tile([P, PACK, n], BF16, name="shared", tag="shared", bufs=2, align_bytes=64)
             nc.scalar.activation(
-                out=shared[c][:, t, :], in_=gelu[c][:, t, 0:n], func=ACT.Copy, scale=chan[:, FG + c, t : t + 1]
+                out=shared[c][:, t, :], in_=gelu[c][:, t, T - n : T], func=ACT.Copy, scale=chan[:, FG + c, t : t + 1]
             )
 
         def vector_gain(c):
             n = share_of(c)
             h_grouped[c] = work.tile([P, T, PACK], BF16, name="h_grouped", tag="h_grouped", bufs=2, align_bytes=64)
-            runs = (T - n) // 4
+            runs = (T - n) // 2
+            if runs == 0:
+                return
             nc.vector.tensor_tensor(
-                out=h_grouped[c][:, n:T, :].rearrange("p (a i) t -> p a t i", i=4),
-                in0=gelu[c][:, :, n:T].rearrange("p t (a i) -> p a t i", i=4),
-                in1=chan[:, FG + c : FG + c + 1, :].unsqueeze(3).to_broadcast([P, runs, PACK, 4]),
+                out=h_grouped[c][:, 0 : T - n, :].rearrange("p (a i) t -> p a t i", i=2),
+                in0=gelu[c][:, :, 0 : T - n].rearrange("p t (a i) -> p a t i", i=2),
+                in1=chan[:, FG + c : FG + c + 1, :].unsqueeze(3).to_broadcast([P, runs, PACK, 2]),
                 op=ALU.mult,
             )
 
@@ -238,16 +258,18 @@ def tile_gelu_feedforward_residual_head_h1_kernel(
             if n == 0:
                 return
             nc.vector.tensor_copy(
-                out=h_grouped[c][:, 0:n, :].rearrange("p (a i) t -> p a t i", i=4),
+                out=h_grouped[c][:, T - n : T, :].rearrange("p (a i) t -> p a t i", i=4),
                 in_=shared[c][:].rearrange("p t (a i) -> p a t i", i=4),
             )
 
         def quantize_h(c):
-            nc.vector.quantize_mx(
-                out=h_codes[c][:].bitcast(FP8X4),
-                scales=h_scales[c][:],
-                in_=h_grouped[c][:].rearrange("p m t -> p (m t)"),
-            )
+            width = T // 2 if c == FG - 1 else T
+            for lo in range(0, T, width):
+                nc.vector.quantize_mx(
+                    out=h_codes[c][:, lo : lo + width].bitcast(FP8X4),
+                    scales=h_scales[c][:, lo : lo + width],
+                    in_=h_grouped[c][:, lo : lo + width, :].rearrange("p m t -> p (m t)"),
+                )
 
         pieces = [(j, h) for j in range(TT) for h in range(DG)]
         rb = {}
@@ -255,17 +277,17 @@ def tile_gelu_feedforward_residual_head_h1_kernel(
         def residual_bias(j, h):
             rb[j, h] = kept("rb%d_%d" % (j, h), [P, KP], F32)
             nc.vector.tensor_tensor(
-                out=rb[j, h][:], in0=st[h][:, j, :], in1=b2_rows[:, h * KP : (h + 1) * KP], op=ALU.add
+                out=rb[j, h][:], in0=st[h, j // 2][:, j % 2, :], in1=b2_rows[:, h * KP : (h + 1) * KP], op=ALU.add
             )
 
         def vector_group(c):
             vector_gain(c)
             interleave_shared(c)
-            if c + LAG < FG:
-                sort_w1(c + LAG)
-            else:
-                first = 3 * (c + LAG - FG)
-                for piece in pieces[first : min(first + 3, 7)]:
+            if c + AHEAD < FG:
+                sort_w1(c + AHEAD)
+            elif c < FG - 1:
+                first = RB_RATE * (c + AHEAD - FG)
+                for piece in pieces[first : first + RB_RATE + (RB_MORE if c == FG - 2 else 0)]:
                     residual_bias(*piece)
             quantize_h(c)
 
@@ -276,12 +298,13 @@ def tile_gelu_feedforward_residual_head_h1_kernel(
             down = [(c - LAG, j, h) for j, h in resident] if not wide else []
             if c == 0:
                 accs = [bank(ring[t]) for t in range(PACK)]
-                for g in range(DG):
-                    for t in range(PACK):
-                        up_pass(accs[t], c, t, g)
+                for t in range(G0):
+                    up_pass(accs[t], c, t, 0)
             for t in range(PACK):
                 if c == 0:
                     acc = accs[t]
+                    for g in range(1 if t < G0 else 0, DG):
+                        up_pass(acc, c, t, g)
                 else:
                     acc = bank(ring[t % len(ring)])
                     for g in range(DG):
@@ -296,82 +319,107 @@ def tile_gelu_feedforward_residual_head_h1_kernel(
                     down_pass(*item)
         scalar_gain(FG - 1, PACK - 1)
         vector_group(FG - 1)
-        residual_bias(*pieces[7])
 
-        for c in range(FG - LAG, FG - 1):
-            for j, h in resident:
-                down_pass(c, j, h)
         late = [(c, j, h) for j, h in pieces[6:] for c in range(FG)]
-        for item in late[:EARLY]:
-            down_pass(*item)
-        for j, h in resident:
-            down_pass(FG - 1, j, h)
-        late = late[EARLY:]
+        marks = [0] * (LAG - 1) + [EARLY_A, EARLY_B]
+        for k in range(LAG):
+            for item in late[marks[k] : marks[k + 1]]:
+                down_pass(*item)
+            for j, h in resident:
+                down_pass(FG - LAG + k, j, h)
+        late = late[EARLY_B:]
 
-        y_codes = kept("y_codes", [P, DG, T], U32)
-        y_scales = kept("y_scales", [P, T], U8)
+        y_codes = [kept("y_codes%d" % pair, [P, DG, 2 * P], U32) for pair in range(TT // 2)]
+        y_scales = kept("y_scales", [P, DG, T], U8)
         words_out = out_1.rearrange("g p m t -> p g (m t)").bitcast(I32)
-        y = {}
+        y = [kept("y%d" % j, [P, D], F32) for j in range(TT)]
         y_pairs = {}
         y_t = {}
         y_grouped = {}
 
         def add_residual(j, h):
-            y[j, h] = kept("y%d_%d" % (j, h), [P, KP], F32)
-            nc.vector.tensor_tensor(out=y[j, h][:], in0=y_acc[j, h][:], in1=rb[j, h][:], op=ALU.add)
-            nc.sync.dma_start(out=out_0[j * P : (j + 1) * P, h * KP : (h + 1) * KP], in_=y[j, h][:])
+            if (j, h) not in rb:
+                residual_bias(j, h)
+            cols = slice(h * KP, (h + 1) * KP)
+            nc.vector.tensor_tensor(out=y[j][:, cols], in0=y_acc[j, h][:], in1=rb[j, h][:], op=ALU.add)
+            if j == TT - 1:
+                nc.sync.dma_start(out=out_0[j * P : (j + 1) * P, cols], in_=y[j][:, cols])
+            elif h == DG - 1:
+                nc.sync.dma_start(out=out_0[j * P : (j + 1) * P, :], in_=y[j][:])
 
-        def round_y(j, h):
-            y_pairs[j, h] = work.tile([P, KP], BF16, name="y_pairs", tag="y_pairs", bufs=4, align_bytes=64)
-            nc.scalar.copy(
-                out=y_pairs[j, h][:].rearrange("p (u m e) -> p u m e", u=2, e=2),
-                in_=y[j, h][:].rearrange("p (m u e) -> p u m e", u=2, e=2),
-            )
+        def by_pairs(ap):
+            return ap.rearrange("p (m u e) -> p u m e", u=2, e=2)
 
-        def turn_y(j, h):
-            y_t[j, h] = bank((2 + 2 * j + h) % 8)
-            words = y_pairs[j, h][:].bitcast(F32)
+        def round_y(j, h, direct):
+            y_pairs[j, h] = kept("y_pairs%d_%d" % (j, h), [P, KP], BF16)
+            dst = y_pairs[j, h][:].rearrange("p (u m e) -> p u m e", u=2, e=2)
+            if direct:
+                nc.vector.tensor_tensor(out=dst, in0=by_pairs(y_acc[j, h][:]), in1=by_pairs(rb[j, h][:]), op=ALU.add)
+            else:
+                nc.scalar.copy(out=dst, in_=by_pairs(y[j][:, h * KP : (h + 1) * KP]))
+
+        def turn_y(j, halves, index):
+            y_t[j, halves] = bank(index)
             for u in range(2):
-                nc.tensor.transpose(y_t[j, h][:, u * P : (u + 1) * P], words[:, u * P : (u + 1) * P], ident[:])
+                for k, h in enumerate(halves):
+                    words = y_pairs[j, h][:].bitcast(F32)
+                    col = (len(halves) * u + k) * P
+                    nc.tensor.transpose(y_t[j, halves][:, col : col + P], words[:, u * P : (u + 1) * P], ident[:])
 
-        def group_y(j, h):
-            y_grouped[j, h] = work.tile([P, KP], BF16, name="y_grouped", tag="y_grouped", bufs=4, align_bytes=64)
+        def group_y(j, halves):
+            n = len(halves)
+            y_grouped[j, halves] = kept("y_grouped%d_%d" % (j, halves[0]), [P, n * KP], BF16)
             nc.scalar.copy(
-                out=y_grouped[j, h][:].bitcast(F32).rearrange("p (r u) -> p r u", u=2),
-                in_=y_t[j, h][:, 0 : 2 * P].rearrange("p (u r) -> p r u", u=2),
+                out=y_grouped[j, halves][:].bitcast(F32).rearrange("p (r u) -> p r u", u=2),
+                in_=y_t[j, halves][:, 0 : 2 * n * P].rearrange("p (u r) -> p r u", u=2),
             )
 
-        def quantize_y(j, h):
-            nc.vector.quantize_mx(
-                out=y_codes[:, h, j * P : (j + 1) * P].bitcast(FP8X4),
-                scales=y_scales[4 * h : P, j * P : (j + 1) * P],
-                in_=y_grouped[j, h][:],
-            )
-            if h == DG - 1:
-                nc.sync.dma_start(
-                    out=words_out[:, :, j * P : (j + 1) * P], in_=y_codes[:, :, j * P : (j + 1) * P].bitcast(I32)
+        def quantize_y(j, halves):
+            for k, h in enumerate(halves):
+                nc.vector.quantize_mx(
+                    out=y_codes[j // 2][:, h, (j % 2) * P : (j % 2 + 1) * P].bitcast(FP8X4),
+                    scales=y_scales[:, h, j * P : (j + 1) * P],
+                    in_=y_grouped[j, halves][:, k * KP : (k + 1) * KP],
                 )
+            if j % 2 == 1 and halves[-1] == DG - 1:
+                nc.sync.dma_start(out=words_out[:, :, (j - 1) * P : (j + 1) * P], in_=y_codes[j // 2][:].bitcast(I32))
 
-        steps = len(pieces)
-        for i in range(steps + 3):
-            if i < steps:
-                j, h = pieces[i]
-                add_residual(j, h)
-                round_y(j, h)
-            if i in (1, 3, 5):
-                count = 4 if i < 5 else len(late)
-                for item in late[:count]:
-                    down_pass(*item)
-                late = late[count:]
-            if 1 <= i <= steps and (i % 2 == 0 or i >= 7):
-                lo = i - 2 if i <= 6 else i - 1
-                for k in range(lo, i):
-                    turn_y(*pieces[k])
-                for k in range(lo, i):
-                    group_y(*pieces[k])
-            if i >= 3:
-                quantize_y(*pieces[i - 3])
+        both = (0, 1)
+        last = TT - 1
+        for j, h in resident[:4]:
+            add_residual(j, h)
+            round_y(j, h, False)
+        for item in late[:STEP]:
+            down_pass(*item)
+        turn_y(0, both, 2)
+        turn_y(1, both, 3)
+        for item in late[STEP:]:
+            down_pass(*item)
+        for j, h in resident[4:]:
+            add_residual(j, h)
+            round_y(j, h, False)
+        group_y(0, both)
+        add_residual(last, 0)
+        round_y(last, 0, False)
+        group_y(1, both)
+        if (last, 1) not in rb:
+            residual_bias(last, 1)
+        quantize_y(0, both)
+        turn_y(2, both, 4)
+        turn_y(last, (0,), 5)
+        round_y(last, 1, True)
+        add_residual(last, 1)
+        turn_y(last, (1,), 6)
+        group_y(2, both)
+        quantize_y(1, both)
+        group_y(last, (0,))
+        group_y(last, (1,))
+        quantize_y(2, both)
+        quantize_y(last, (0,))
+        quantize_y(last, (1,))
         for q in range(4):
-            nc.sync.dma_start(
-                out=out_2[:, 4 * q : 4 * q + 4, :].bitcast(I32), in_=y_scales[32 * q : 32 * q + 8, :].bitcast(I32)
+            queue = nc.sync if q % 2 == 0 else nc.scalar
+            queue.dma_start(
+                out=out_2[:, 4 * q : 4 * q + 4, :].rearrange("g r n -> r g n").bitcast(I32),
+                in_=y_scales[32 * q : 32 * q + 4, :, :].bitcast(I32),
             )

@@ -23,15 +23,20 @@ DG = D // KP
 FG = F // KP
 TT = T // P
 LAG = 3
-SHARE = 320
+SHARE = 288
 SHARE_FROM = 2
 SHARE_LAST = 256
 EARLY_A = 0
-EARLY_B = 2
+EARLY_B = 3
 STEP = 6
 AHEAD = 4
 RB_RATE = 2
 XORD = 0
+W1FIRST = 0
+RES = 6
+MID = 0
+WALK = 4
+WARM = 0
 RB_MORE = 0
 G0 = 2
 
@@ -56,35 +61,33 @@ def tile_gelu_feedforward_residual_head_h1_kernel(
         make_identity(nc, ident[:])
         vec = kept("vec", [P, KP], BF16)
         nc.vector.memset(vec[:].bitcast(I32), 0)
-        nc.scalar.dma_start(out=vec[2 * FG : 2 * FG + DG, :], in_=in_scale.rearrange("(g n) -> g n", n=KP))
-        nc.scalar.dma_start(out=vec[0:FG, :], in_=b1.rearrange("(g n) -> g n", n=KP))
-        nc.scalar.dma_start(out=vec[FG : 2 * FG, :], in_=mid_scale.rearrange("(g n) -> g n", n=KP))
-        warm = kept("warm", [P, 2], F32)
-        nc.vector.memset(warm[:, 0:1], 0.0)
-        nc.scalar.activation(out=warm[:, 1:2], in_=warm[:, 0:1], func=ACT.Gelu_apprx_tanh)
+        if WARM:
+            warm = kept("warm", [P, 2], F32)
+            nc.vector.memset(warm[:, 0:1], 0.0)
+            nc.scalar.activation(out=warm[:, 1:2], in_=warm[:, 0:1], func=ACT.Gelu_apprx_tanh)
         plane1 = [kept("plane1_%d" % g, [P, FG, KP], U8) for g in range(DG)]
         plane2 = kept("plane2", [P, FG, D], U8)
-        for tile in plane1:
+        for tile in plane1 + [plane2]:
             nc.vector.memset(tile[:].rearrange("p c n -> p (c n)").bitcast(I32), 0)
-        nc.gpsimd.memset(plane2[:].rearrange("p c n -> p (c n)").bitcast(I32), 0)
 
-        s1_raw = kept("s1_raw", [P, DG, KP], U8)
-        nc.sync.dma_start(
-            out=s1_raw[:].bitcast(I32),
-            in_=w1_scales.rearrange("g q (c n) -> (q c) g n", c=FG).bitcast(I32),
-        )
+        s1_raw = kept("s1_raw", [P, 2 * KP], U8)
+        by_row = w1_scales.rearrange("g (q r) n -> r (g q) n", r=4)
+        for r in range(4):
+            nc.sync.dma_start(out=s1_raw[32 * r : 32 * r + 32, :].bitcast(I32), in_=by_row[r].bitcast(I32))
+        x_gain = kept("x_gain", [P, DG, PACK], BF16)
+        nc.scalar.dma_start(out=x_gain[:], in_=in_scale.rearrange("(g p t) -> p g t", p=P, t=PACK))
 
         def place_s1():
-            tile = kept("s1_sorted", [P, DG, KP], U8)
+            tile = kept("s1_sorted", [P, 2 * KP], U8)
             nc.vector.tensor_copy(
-                out=tile[:].rearrange("p g (t m) -> p g t m", t=PACK),
-                in_=s1_raw[:].rearrange("p g (m t) -> p g t m", t=PACK),
+                out=tile[:].rearrange("p (c t m) -> p c t m", c=2, t=PACK),
+                in_=s1_raw[:].rearrange("p (c m t) -> p c t m", c=2, t=PACK),
             )
             for g in range(DG):
-                for q in range(4):
+                for r in range(4):
                     nc.sync.dma_start(
-                        out=plane1[g][32 * q : 32 * q + 4, :, :].bitcast(I32),
-                        in_=tile[32 * q : 32 * q + 32, g, :].bitcast(I32),
+                        out=plane1[g][r:P:32, :, :].rearrange("p c n -> p (c n)").bitcast(I32),
+                        in_=tile[32 * r + 16 * g : 32 * r + 16 * (g + 1), :].bitcast(I32),
                     )
 
         st = {}
@@ -114,23 +117,24 @@ def tile_gelu_feedforward_residual_head_h1_kernel(
         for g in range(DG):
             for half in range(2):
                 load_states(g, half)
+        nc.scalar.dma_start(out=vec[0:FG, :], in_=b1.rearrange("(g n) -> g n", n=KP))
+        nc.scalar.dma_start(out=vec[FG : 2 * FG, :], in_=mid_scale.rearrange("(g n) -> g n", n=KP))
+        if W1FIRST:
+            load_w1(1)
         place_s1()
-        load_w1(1)
-        load_w1(2)
-        load_w1(3)
-        for q in range(4):
+        for c in range(1 + W1FIRST, AHEAD + 1):
+            load_w1(c)
+        for r in range(4):
             nc.sync.dma_start(
-                out=plane2[32 * q : 32 * q + 4, :, :].bitcast(I32),
-                in_=w2_scales[:, 4 * q : 4 * q + 4, :].rearrange("g r n -> r g n").bitcast(I32),
+                out=plane2[r:P:32, :, :].bitcast(I32),
+                in_=w2_scales[:, r:16:4, :].rearrange("g q n -> q g n").bitcast(I32),
             )
         load_w2(0)
-        load_w1(4)
-        load_w2(1)
-        load_w1(5)
-        load_w1(6)
-        load_w2(2)
-        load_w1(7)
-        load_w2(3)
+        for c in range(AHEAD + 1, FG):
+            load_w1(c)
+            load_w2(len(w2))
+        for pair in range(len(w2), FG // 2):
+            load_w2(pair)
         b2_rows = kept("b2_rows", [P, D], BF16)
         nc.sync.dma_start(out=b2_rows[:], in_=b2.partition_broadcast(P))
 
@@ -138,13 +142,13 @@ def tile_gelu_feedforward_residual_head_h1_kernel(
             for u in range(2):
                 nc.tensor.transpose(dst[u], src_words[:, u::2], ident[:])
 
-        vec_t = bank(0)
-        word_transposes([vec_t[:, u * P : (u + 1) * P] for u in range(2)], vec[:].bitcast(F32))
-        vec_view = vec_t[:, 0 : 2 * P].bitcast(BF16).rearrange("p (u r e) -> p r u e", u=2, e=2)
-        x_gain = kept("x_gain", [P, DG, PACK], BF16)
-        nc.scalar.copy(out=x_gain[:].rearrange("p r (u e) -> p r u e", e=2), in_=vec_view[:, 2 * FG : 2 * FG + DG])
         chan = kept("chan", [P, 2 * FG, PACK], F32)
-        nc.scalar.copy(out=chan[:].rearrange("p r (u e) -> p r u e", e=2), in_=vec_view[:, 0 : 2 * FG])
+
+        def place_vectors():
+            vec_t = bank(3)
+            word_transposes([vec_t[:, u * P : (u + 1) * P] for u in range(2)], vec[:].bitcast(F32))
+            vec_view = vec_t[:, 0 : 2 * P].bitcast(BF16).rearrange("p (u r e) -> p r u e", u=2, e=2)
+            nc.vector.tensor_copy(out=chan[:].rearrange("p r (u e) -> p r u e", e=2), in_=vec_view[:, 0 : 2 * FG])
 
         w1 = []
 
@@ -163,7 +167,7 @@ def tile_gelu_feedforward_residual_head_h1_kernel(
         x_scales = [kept("x_scales%d" % g, [P, T], U8) for g in range(DG)]
 
         def x_half(g, half):
-            acc = bank(2 + 2 * g + half)
+            acc = bank(4 + 2 * g + half)
             for jj in range(2):
                 words = st[g, half][:, jj, :].bitcast(F32)
                 word_transposes([acc[:, (2 * u + jj) * P : (2 * u + jj + 1) * P] for u in range(2)], words)
@@ -186,6 +190,7 @@ def tile_gelu_feedforward_residual_head_h1_kernel(
             x_half(1, 0)
             quantize_x(0)
         x_half(1, 1)
+        place_vectors()
         quantize_x(1)
         for c in range(1, AHEAD):
             sort_w1(c)
@@ -207,7 +212,7 @@ def tile_gelu_feedforward_residual_head_h1_kernel(
 
         def down_pass(c, j, h):
             if c == 0:
-                y_acc[j, h] = bank((2 + 2 * j + h) % 8)
+                y_acc[j, h] = bank(home[j, h])
             nc.tensor.matmul_mx(
                 out=y_acc[j, h][:],
                 lhsT=h_codes[c][:, j * P : (j + 1) * P].bitcast(FP8X4),
@@ -243,13 +248,13 @@ def tile_gelu_feedforward_residual_head_h1_kernel(
         def vector_gain(c):
             n = share_of(c)
             h_grouped[c] = work.tile([P, T, PACK], BF16, name="h_grouped", tag="h_grouped", bufs=2, align_bytes=64)
-            runs = (T - n) // 2
+            runs = (T - n) // WALK
             if runs == 0:
                 return
             nc.vector.tensor_tensor(
-                out=h_grouped[c][:, 0 : T - n, :].rearrange("p (a i) t -> p a t i", i=2),
-                in0=gelu[c][:, :, 0 : T - n].rearrange("p t (a i) -> p a t i", i=2),
-                in1=chan[:, FG + c : FG + c + 1, :].unsqueeze(3).to_broadcast([P, runs, PACK, 2]),
+                out=h_grouped[c][:, 0 : T - n, :].rearrange("p (a i) t -> p a t i", i=WALK),
+                in0=gelu[c][:, :, 0 : T - n].rearrange("p t (a i) -> p a t i", i=WALK),
+                in1=chan[:, FG + c : FG + c + 1, :].unsqueeze(3).to_broadcast([P, runs, PACK, WALK]),
                 op=ALU.mult,
             )
 
@@ -291,13 +296,17 @@ def tile_gelu_feedforward_residual_head_h1_kernel(
                     residual_bias(*piece)
             quantize_h(c)
 
-        resident = pieces[:6]
+        resident = pieces[:RES]
+        narrow = 8 - RES
+        slots = (FG - LAG) * PACK
+        home = dict(zip(resident, [4, 5, 6, 7, 3, 2]))
+        for k, piece in enumerate(pieces[RES:]):
+            home[piece] = (slots + k) % narrow
         for c in range(FG):
             wide = c < LAG
-            ring = [0, 1, 6, 7] if wide else [0, 1]
             down = [(c - LAG, j, h) for j, h in resident] if not wide else []
             if c == 0:
-                accs = [bank(ring[t]) for t in range(PACK)]
+                accs = [bank(t) for t in range(PACK)]
                 for t in range(G0):
                     up_pass(accs[t], c, t, 0)
             for t in range(PACK):
@@ -306,7 +315,7 @@ def tile_gelu_feedforward_residual_head_h1_kernel(
                     for g in range(1 if t < G0 else 0, DG):
                         up_pass(acc, c, t, g)
                 else:
-                    acc = bank(ring[t % len(ring)])
+                    acc = bank(t if wide else ((c - LAG) * PACK + t) % narrow)
                     for g in range(DG):
                         up_pass(acc, c, t, g)
                 gelu_out(c, t, acc)
@@ -315,12 +324,12 @@ def tile_gelu_feedforward_residual_head_h1_kernel(
                 elif c > 0:
                     scalar_gain(c - 1, PACK - 1)
                     vector_group(c - 1)
-                for item in down[(3 * t + 1) // 2 : (3 * t + 4) // 2]:
+                for item in down[(RES * t + 2) // PACK : (RES * (t + 1) + 2) // PACK]:
                     down_pass(*item)
         scalar_gain(FG - 1, PACK - 1)
         vector_group(FG - 1)
 
-        late = [(c, j, h) for j, h in pieces[6:] for c in range(FG)]
+        late = [(c, j, h) for j, h in pieces[RES:] for c in range(FG)]
         marks = [0] * (LAG - 1) + [EARLY_A, EARLY_B]
         for k in range(LAG):
             for item in late[marks[k] : marks[k + 1]]:
@@ -391,8 +400,8 @@ def tile_gelu_feedforward_residual_head_h1_kernel(
             round_y(j, h, False)
         for item in late[:STEP]:
             down_pass(*item)
-        turn_y(0, both, 2)
-        turn_y(1, both, 3)
+        turn_y(0, both, 4)
+        turn_y(1, both, 5)
         for item in late[STEP:]:
             down_pass(*item)
         for j, h in resident[4:]:
@@ -402,14 +411,13 @@ def tile_gelu_feedforward_residual_head_h1_kernel(
         add_residual(last, 0)
         round_y(last, 0, False)
         group_y(1, both)
-        if (last, 1) not in rb:
-            residual_bias(last, 1)
+        residual_bias(last, 1)
         quantize_y(0, both)
-        turn_y(2, both, 4)
-        turn_y(last, (0,), 5)
+        turn_y(2, both, 6)
+        turn_y(last, (0,), 7)
         round_y(last, 1, True)
         add_residual(last, 1)
-        turn_y(last, (1,), 6)
+        turn_y(last, (1,), 3)
         group_y(2, both)
         quantize_y(1, both)
         group_y(last, (0,))
@@ -420,6 +428,6 @@ def tile_gelu_feedforward_residual_head_h1_kernel(
         for q in range(4):
             queue = nc.sync if q % 2 == 0 else nc.scalar
             queue.dma_start(
-                out=out_2[:, 4 * q : 4 * q + 4, :].rearrange("g r n -> r g n").bitcast(I32),
-                in_=y_scales[32 * q : 32 * q + 4, :, :].bitcast(I32),
+                out=out_2[:, q:16:4, :].rearrange("g r n -> r g n").bitcast(I32),
+                in_=y_scales[q:P:32, :, :].bitcast(I32),
             )

@@ -18,27 +18,30 @@ ACT = mybir.ActivationFunctionType
 
 P = 128
 PACK = 4
-KP = P * PACK
-DG = D // KP
-FG = F // KP
-TT = T // P
-LAG = 3
-SHARE = 288
+GROUP = P * PACK
+QUAD = 32
+SCALE_ROWS = 4
+BLOCKS = GROUP // 32
+D_GROUPS = D // GROUP
+F_GROUPS = F // GROUP
+TOKEN_TILES = T // P
+ALIGN = 64
+RUN = 4
+
+DOWN_LAG = 3
+SORT_AHEAD = 4
+
 SHARE_FROM = 2
-SHARE_LAST = 256
-EARLY_A = 0
-EARLY_B = 3
-STEP = 6
-AHEAD = 4
-RB_RATE = 2
-XORD = 0
-W1FIRST = 0
-RES = 6
-MID = 0
-WALK = 4
-WARM = 0
-RB_MORE = 0
-G0 = 2
+SCALAR_TOKENS = 304
+HALF_TOKENS = T // 2
+
+WIDE_RING = 4
+NARROW_RING = 2
+X_BANKS = 4
+VECTOR_BANK = 3
+RESIDENT_BANKS = [4, 5, 6, 7, 3, 2]
+LATE_BEFORE_LAST_GROUP = 3
+LATE_BEFORE_TURNS = 6
 
 
 def tile_gelu_feedforward_residual_head_h1_kernel(
@@ -52,163 +55,156 @@ def tile_gelu_feedforward_residual_head_h1_kernel(
         ctx.enter_context(tc.manual_schedule())
 
         def kept(name, shape, dtype):
-            return keep.tile(shape, dtype, name=name, tag=name, align_bytes=64)
+            return keep.tile(shape, dtype, name=name, tag=name, align_bytes=ALIGN)
 
         def bank(index):
-            return psum.tile([P, KP], F32, name="bank%d" % index, tag="bank%d" % index)
+            return psum.tile([P, GROUP], F32, name="bank%d" % index, tag="bank%d" % index)
 
         ident = kept("ident", [P, P], F32)
         make_identity(nc, ident[:])
-        vec = kept("vec", [P, KP], BF16)
-        nc.vector.memset(vec[:].bitcast(I32), 0)
-        if WARM:
-            warm = kept("warm", [P, 2], F32)
-            nc.vector.memset(warm[:, 0:1], 0.0)
-            nc.scalar.activation(out=warm[:, 1:2], in_=warm[:, 0:1], func=ACT.Gelu_apprx_tanh)
-        plane1 = [kept("plane1_%d" % g, [P, FG, KP], U8) for g in range(DG)]
-        plane2 = kept("plane2", [P, FG, D], U8)
-        for tile in plane1 + [plane2]:
-            nc.vector.memset(tile[:].rearrange("p c n -> p (c n)").bitcast(I32), 0)
+        vector_rows = kept("vector_rows", [P, GROUP], BF16)
+        nc.vector.memset(vector_rows[:].bitcast(I32), 0)
+        w1_planes = [kept("w1_plane%d" % g, [P, F_GROUPS, GROUP], U8) for g in range(D_GROUPS)]
+        w2_plane = kept("w2_plane", [P, F_GROUPS, D], U8)
+        for plane in w1_planes + [w2_plane]:
+            nc.vector.memset(plane[:].rearrange("p c n -> p (c n)").bitcast(I32), 0)
 
-        s1_raw = kept("s1_raw", [P, 2 * KP], U8)
-        by_row = w1_scales.rearrange("g (q r) n -> r (g q) n", r=4)
-        for r in range(4):
-            nc.sync.dma_start(out=s1_raw[32 * r : 32 * r + 32, :].bitcast(I32), in_=by_row[r].bitcast(I32))
-        x_gain = kept("x_gain", [P, DG, PACK], BF16)
+        dense_cols = D_GROUPS * BLOCKS * F // P
+        w1_dense = kept("w1_dense", [P, dense_cols], U8)
+        by_row = w1_scales.rearrange("g (q r) n -> r (g q) n", r=SCALE_ROWS)
+        for r in range(SCALE_ROWS):
+            nc.sync.dma_start(out=w1_dense[QUAD * r : QUAD * (r + 1), :].bitcast(I32), in_=by_row[r].bitcast(I32))
+        x_gain = kept("x_gain", [P, D_GROUPS, PACK], BF16)
         nc.scalar.dma_start(out=x_gain[:], in_=in_scale.rearrange("(g p t) -> p g t", p=P, t=PACK))
-
-        def place_s1():
-            tile = kept("s1_sorted", [P, 2 * KP], U8)
-            nc.vector.tensor_copy(
-                out=tile[:].rearrange("p (c t m) -> p c t m", c=2, t=PACK),
-                in_=s1_raw[:].rearrange("p (c m t) -> p c t m", c=2, t=PACK),
-            )
-            for g in range(DG):
-                for r in range(4):
-                    nc.sync.dma_start(
-                        out=plane1[g][r:P:32, :, :].rearrange("p c n -> p (c n)").bitcast(I32),
-                        in_=tile[32 * r + 16 * g : 32 * r + 16 * (g + 1), :].bitcast(I32),
-                    )
-
-        st = {}
-
-        def load_states(g, half):
-            st[g, half] = kept("st%d_%d" % (g, half), [P, 2, KP], BF16)
-            src = states[half * 2 * P : (half + 1) * 2 * P, g * KP : (g + 1) * KP]
-            nc.sync.dma_start(out=st[g, half][:], in_=src.rearrange("(j p) n -> p j n", p=P))
 
         w1_raw = []
 
         def load_w1(c):
-            tile = kept("w1_raw%d" % c, [P, DG, 2 * KP], U8)
-            src = w1_words[:, :, 2 * KP * c : 2 * KP * (c + 1)].rearrange("g p n -> p g n")
-            nc.sync.dma_start(out=tile[:].bitcast(I32), in_=src.bitcast(I32))
-            w1_raw.append(tile)
+            raw = kept("w1_raw%d" % c, [P, D_GROUPS, 2 * GROUP], U8)
+            src = w1_words[:, :, 2 * GROUP * c : 2 * GROUP * (c + 1)].rearrange("g p n -> p g n")
+            nc.sync.dma_start(out=raw[:].bitcast(I32), in_=src.bitcast(I32))
+            w1_raw.append(raw)
 
         w2 = []
 
         def load_w2(pair):
-            tile = kept("w2_%d" % pair, [P, 2, 2 * D], U8)
+            words = kept("w2_%d" % pair, [P, 2, 2 * D], U8)
             src = w2_words[2 * pair : 2 * pair + 2].rearrange("g p n -> p g n")
-            nc.sync.dma_start(out=tile[:].bitcast(I32), in_=src.bitcast(I32))
-            w2.append(tile)
+            nc.sync.dma_start(out=words[:].bitcast(I32), in_=src.bitcast(I32))
+            w2.append(words)
 
         load_w1(0)
-        for g in range(DG):
+        rows = {}
+        for g in range(D_GROUPS):
             for half in range(2):
-                load_states(g, half)
-        nc.scalar.dma_start(out=vec[0:FG, :], in_=b1.rearrange("(g n) -> g n", n=KP))
-        nc.scalar.dma_start(out=vec[FG : 2 * FG, :], in_=mid_scale.rearrange("(g n) -> g n", n=KP))
-        if W1FIRST:
-            load_w1(1)
-        place_s1()
-        for c in range(1 + W1FIRST, AHEAD + 1):
+                rows[g, half] = kept("rows%d_%d" % (g, half), [P, 2, GROUP], BF16)
+                src = states[half * HALF_TOKENS : (half + 1) * HALF_TOKENS, g * GROUP : (g + 1) * GROUP]
+                nc.sync.dma_start(out=rows[g, half][:], in_=src.rearrange("(j p) n -> p j n", p=P))
+        nc.scalar.dma_start(out=vector_rows[0:F_GROUPS, :], in_=b1.rearrange("(c n) -> c n", n=GROUP))
+        nc.scalar.dma_start(
+            out=vector_rows[F_GROUPS : 2 * F_GROUPS, :], in_=mid_scale.rearrange("(c n) -> c n", n=GROUP)
+        )
+        load_w1(1)
+
+        w1_dense_sorted = kept("w1_dense_sorted", [P, dense_cols], U8)
+        nc.vector.tensor_copy(
+            out=w1_dense_sorted[:].rearrange("p (c t m) -> p c t m", t=PACK, m=P),
+            in_=w1_dense[:].rearrange("p (c m t) -> p c t m", t=PACK, m=P),
+        )
+        per_group = QUAD // D_GROUPS
+        for g in range(D_GROUPS):
+            for r in range(SCALE_ROWS):
+                first = QUAD * r + per_group * g
+                nc.sync.dma_start(
+                    out=w1_planes[g][r:P:QUAD, :, :].rearrange("p c n -> p (c n)").bitcast(I32),
+                    in_=w1_dense_sorted[first : first + per_group, :].bitcast(I32),
+                )
+        for c in range(2, SORT_AHEAD + 1):
             load_w1(c)
-        for r in range(4):
+        for r in range(SCALE_ROWS):
             nc.sync.dma_start(
-                out=plane2[r:P:32, :, :].bitcast(I32),
-                in_=w2_scales[:, r:16:4, :].rearrange("g q n -> q g n").bitcast(I32),
+                out=w2_plane[r:P:QUAD, :, :].bitcast(I32),
+                in_=w2_scales[:, r:BLOCKS:SCALE_ROWS, :].rearrange("c q n -> q c n").bitcast(I32),
             )
         load_w2(0)
-        for c in range(AHEAD + 1, FG):
+        for c in range(SORT_AHEAD + 1, F_GROUPS):
             load_w1(c)
-            load_w2(len(w2))
-        for pair in range(len(w2), FG // 2):
-            load_w2(pair)
+            load_w2(c - SORT_AHEAD)
         b2_rows = kept("b2_rows", [P, D], BF16)
         nc.sync.dma_start(out=b2_rows[:], in_=b2.partition_broadcast(P))
 
-        def word_transposes(dst, src_words):
-            for u in range(2):
-                nc.tensor.transpose(dst[u], src_words[:, u::2], ident[:])
+        w1 = [kept("w1_%d" % c, [P, D_GROUPS, PACK, 2 * P], U8) for c in range(F_GROUPS)]
 
-        chan = kept("chan", [P, 2 * FG, PACK], F32)
-
-        def place_vectors():
-            vec_t = bank(3)
-            word_transposes([vec_t[:, u * P : (u + 1) * P] for u in range(2)], vec[:].bitcast(F32))
-            vec_view = vec_t[:, 0 : 2 * P].bitcast(BF16).rearrange("p (u r e) -> p r u e", u=2, e=2)
-            nc.vector.tensor_copy(out=chan[:].rearrange("p r (u e) -> p r u e", e=2), in_=vec_view[:, 0 : 2 * FG])
-
-        w1 = []
-
-        def sort_w1(c):
-            tile = kept("w1_%d" % c, [P, DG, PACK, 2 * P], U8)
+        def sort_w1(c, groups):
             nc.vector.tensor_copy(
-                out=tile[:].rearrange("p g t (m b) -> p g t m b", b=2),
-                in_=w1_raw[c][:].rearrange("p g (m t b) -> p g t m b", t=PACK, b=2),
+                out=w1[c][:, groups].rearrange("p g t (m b) -> p g t m b", b=2),
+                in_=w1_raw[c][:, groups].rearrange("p g (m t b) -> p g t m b", t=PACK, b=2),
             )
-            w1.append(tile)
 
-        sort_w1(0)
+        def turn_words(src, acc, col, stride):
+            words = src.bitcast(F32)
+            for u in range(2):
+                nc.tensor.transpose(acc[:, col + u * stride : col + u * stride + P], words[:, u::2], ident[:])
 
-        x_grouped = [kept("x_grouped%d" % g, [P, T * PACK], BF16) for g in range(DG)]
-        x_codes = [kept("x_codes%d" % g, [P, T], U32) for g in range(DG)]
-        x_scales = [kept("x_scales%d" % g, [P, T], U8) for g in range(DG)]
+        x_grouped = [kept("x_grouped%d" % g, [P, T * PACK], BF16) for g in range(D_GROUPS)]
+        x_codes = [kept("x_codes%d" % g, [P, T], U32) for g in range(D_GROUPS)]
+        x_scales = [kept("x_scales%d" % g, [P, T], U8) for g in range(D_GROUPS)]
 
-        def x_half(g, half):
-            acc = bank(4 + 2 * g + half)
-            for jj in range(2):
-                words = st[g, half][:, jj, :].bitcast(F32)
-                word_transposes([acc[:, (2 * u + jj) * P : (2 * u + jj + 1) * P] for u in range(2)], words)
+        def scale_x(g, half):
+            acc = bank(X_BANKS + 2 * g + half)
+            for tile in range(2):
+                turn_words(rows[g, half][:, tile, :], acc, tile * P, HALF_TOKENS)
+            cols = slice(half * HALF_TOKENS * PACK, (half + 1) * HALF_TOKENS * PACK)
+            gain = x_gain[:, g : g + 1, :].rearrange("p o (u e) -> p o u e", e=2)
             nc.vector.tensor_tensor(
-                out=x_grouped[g][:, half * 1024 : (half + 1) * 1024].rearrange("p (r u e) -> p r u e", u=2, e=2),
-                in0=acc[:].bitcast(BF16).rearrange("p (u r e) -> p r u e", u=2, e=2),
-                in1=x_gain[:, g : g + 1, :].rearrange("p o (u e) -> p o u e", e=2).to_broadcast([P, 2 * P, 2, 2]),
+                out=x_grouped[g][:, cols].rearrange("p (m u e) -> p m u e", u=2, e=2),
+                in0=acc[:].bitcast(BF16).rearrange("p (u m e) -> p m u e", u=2, e=2),
+                in1=gain.to_broadcast([P, HALF_TOKENS, 2, 2]),
                 op=ALU.mult,
             )
 
         def quantize_x(g):
             nc.vector.quantize_mx(out=x_codes[g][:].bitcast(FP8X4), scales=x_scales[g][:], in_=x_grouped[g][:])
 
-        x_half(0, 0)
-        x_half(0, 1)
-        if XORD:
-            quantize_x(0)
-            x_half(1, 0)
-        else:
-            x_half(1, 0)
-            quantize_x(0)
-        x_half(1, 1)
-        place_vectors()
+        all_groups = slice(0, D_GROUPS)
+        sort_w1(0, all_groups)
+        scale_x(0, 0)
+        scale_x(0, 1)
+        scale_x(1, 0)
+        quantize_x(0)
+        scale_x(1, 1)
+        channel = kept("channel", [P, 2 * F_GROUPS, PACK], F32)
+        turned = bank(VECTOR_BANK)
+        turn_words(vector_rows[:], turned, 0, P)
+        turned_values = turned[:, 0 : 2 * P].bitcast(BF16).rearrange("p (u c e) -> p c u e", u=2, e=2)
+        nc.vector.tensor_copy(
+            out=channel[:].rearrange("p c (u e) -> p c u e", e=2), in_=turned_values[:, 0 : 2 * F_GROUPS]
+        )
         quantize_x(1)
-        for c in range(1, AHEAD):
-            sort_w1(c)
+        for c in range(1, SORT_AHEAD):
+            sort_w1(c, all_groups)
+
+        pieces = [(j, h) for j in range(TOKEN_TILES) for h in range(D_GROUPS)]
+        resident = pieces[: len(RESIDENT_BANKS)]
+        late_pieces = pieces[len(RESIDENT_BANKS) :]
+        home = dict(zip(pieces, RESIDENT_BANKS + list(range(NARROW_RING))))
+        h_codes = [kept("h_codes%d" % c, [P, T], U32) for c in range(F_GROUPS)]
+        h_scales = [kept("h_scales%d" % c, [P, T], U8) for c in range(F_GROUPS)]
+        gelu = {}
+        scalar_part = {}
+        y_acc = {}
+        base = {}
 
         def up_pass(acc, c, t, g):
             nc.tensor.matmul_mx(
                 out=acc[:],
                 lhsT=w1[c][:, g, t, :].bitcast(FP4X4),
-                lhsT_scale=plane1[g][:, c, t * P : (t + 1) * P],
+                lhsT_scale=w1_planes[g][:, c, t * P : (t + 1) * P],
                 rhs=x_codes[g][:].bitcast(FP8X4),
                 rhs_scale=x_scales[g][:],
                 start=(g == 0),
-                stop=(g == DG - 1),
+                stop=(g == D_GROUPS - 1),
             )
-
-        h_codes = [kept("h_codes%d" % c, [P, T], U32) for c in range(FG)]
-        h_scales = [kept("h_scales%d" % c, [P, T], U8) for c in range(FG)]
-        y_acc = {}
 
         def down_pass(c, j, h):
             if c == 0:
@@ -217,217 +213,212 @@ def tile_gelu_feedforward_residual_head_h1_kernel(
                 out=y_acc[j, h][:],
                 lhsT=h_codes[c][:, j * P : (j + 1) * P].bitcast(FP8X4),
                 lhsT_scale=h_scales[c][:, j * P : (j + 1) * P],
-                rhs=w2[c // 2][:, c % 2, 2 * KP * h : 2 * KP * (h + 1)].bitcast(FP4X4),
-                rhs_scale=plane2[:, c, KP * h : KP * (h + 1)],
+                rhs=w2[c // 2][:, c % 2, 2 * GROUP * h : 2 * GROUP * (h + 1)].bitcast(FP4X4),
+                rhs_scale=w2_plane[:, c, GROUP * h : GROUP * (h + 1)],
                 start=(c == 0),
-                stop=(c == FG - 1),
+                stop=(c == F_GROUPS - 1),
             )
 
-        gelu = {}
-        shared = {}
-        h_grouped = {}
+        def scalar_tokens(c):
+            if c == F_GROUPS - 1:
+                return HALF_TOKENS
+            return SCALAR_TOKENS if c >= SHARE_FROM else 0
 
-        def share_of(c):
-            return SHARE_LAST if c == FG - 1 else SHARE if c >= SHARE_FROM else 0
-
-        def gelu_out(c, t, acc):
+        def apply_gelu(c, t, acc):
             if t == 0:
-                gelu[c] = work.tile([P, PACK, T], F32, name="gelu", tag="gelu", bufs=4, align_bytes=64)
-            nc.scalar.activation(out=gelu[c][:, t, :], in_=acc[:], func=ACT.Gelu_apprx_tanh, bias=chan[:, c, t : t + 1])
+                gelu[c] = work.tile(
+                    [P, PACK, T], F32, name="gelu", tag="gelu", bufs=DOWN_LAG + 1, align_bytes=ALIGN
+                )
+            nc.scalar.activation(
+                out=gelu[c][:, t, :], in_=acc[:], func=ACT.Gelu_apprx_tanh, bias=channel[:, c, t : t + 1]
+            )
 
-        def scalar_gain(c, t):
-            n = share_of(c)
+        def gain_on_scalar(c, t):
+            n = scalar_tokens(c)
             if n == 0:
                 return
             if t == 0:
-                shared[c] = work.tile([P, PACK, n], BF16, name="shared", tag="shared", bufs=2, align_bytes=64)
+                scalar_part[c] = work.tile(
+                    [P, PACK, n], BF16, name="scalar_part", tag="scalar_part", align_bytes=ALIGN
+                )
             nc.scalar.activation(
-                out=shared[c][:, t, :], in_=gelu[c][:, t, T - n : T], func=ACT.Copy, scale=chan[:, FG + c, t : t + 1]
+                out=scalar_part[c][:, t, :],
+                in_=gelu[c][:, t, T - n : T],
+                func=ACT.Copy,
+                scale=channel[:, F_GROUPS + c, t : t + 1],
             )
 
-        def vector_gain(c):
-            n = share_of(c)
-            h_grouped[c] = work.tile([P, T, PACK], BF16, name="h_grouped", tag="h_grouped", bufs=2, align_bytes=64)
-            runs = (T - n) // WALK
-            if runs == 0:
-                return
+        def add_base(j, h):
+            base[j, h] = kept("base%d_%d" % (j, h), [P, GROUP], F32)
             nc.vector.tensor_tensor(
-                out=h_grouped[c][:, 0 : T - n, :].rearrange("p (a i) t -> p a t i", i=WALK),
-                in0=gelu[c][:, :, 0 : T - n].rearrange("p t (a i) -> p a t i", i=WALK),
-                in1=chan[:, FG + c : FG + c + 1, :].unsqueeze(3).to_broadcast([P, runs, PACK, WALK]),
+                out=base[j, h][:],
+                in0=rows[h, j // 2][:, j % 2, :],
+                in1=b2_rows[:, h * GROUP : (h + 1) * GROUP],
+                op=ALU.add,
+            )
+
+        def finish_h(c):
+            n = scalar_tokens(c)
+            grouped = work.tile([P, T, PACK], BF16, name="h_grouped", tag="h_grouped", align_bytes=ALIGN)
+            gain = channel[:, F_GROUPS + c : F_GROUPS + c + 1, :].unsqueeze(3)
+            nc.vector.tensor_tensor(
+                out=grouped[:, 0 : T - n, :].rearrange("p (a i) t -> p a t i", i=RUN),
+                in0=gelu[c][:, :, 0 : T - n].rearrange("p t (a i) -> p a t i", i=RUN),
+                in1=gain.to_broadcast([P, (T - n) // RUN, PACK, RUN]),
                 op=ALU.mult,
             )
-
-        def interleave_shared(c):
-            n = share_of(c)
-            if n == 0:
-                return
-            nc.vector.tensor_copy(
-                out=h_grouped[c][:, T - n : T, :].rearrange("p (a i) t -> p a t i", i=4),
-                in_=shared[c][:].rearrange("p t (a i) -> p a t i", i=4),
-            )
-
-        def quantize_h(c):
-            width = T // 2 if c == FG - 1 else T
-            for lo in range(0, T, width):
-                nc.vector.quantize_mx(
-                    out=h_codes[c][:, lo : lo + width].bitcast(FP8X4),
-                    scales=h_scales[c][:, lo : lo + width],
-                    in_=h_grouped[c][:, lo : lo + width, :].rearrange("p m t -> p (m t)"),
+            if n > 0:
+                nc.vector.tensor_copy(
+                    out=grouped[:, T - n : T, :].rearrange("p (a i) t -> p a t i", i=RUN),
+                    in_=scalar_part[c][:].rearrange("p t (a i) -> p a t i", i=RUN),
                 )
 
-        pieces = [(j, h) for j in range(TT) for h in range(DG)]
-        rb = {}
+            def quantize_h(lo, hi):
+                nc.vector.quantize_mx(
+                    out=h_codes[c][:, lo:hi].bitcast(FP8X4),
+                    scales=h_scales[c][:, lo:hi],
+                    in_=grouped[:, lo:hi, :].rearrange("p m t -> p (m t)"),
+                )
 
-        def residual_bias(j, h):
-            rb[j, h] = kept("rb%d_%d" % (j, h), [P, KP], F32)
-            nc.vector.tensor_tensor(
-                out=rb[j, h][:], in0=st[h, j // 2][:, j % 2, :], in1=b2_rows[:, h * KP : (h + 1) * KP], op=ALU.add
-            )
+            ahead = c + SORT_AHEAD
+            if ahead < F_GROUPS:
+                sort_w1(ahead, slice(0, 1))
+                quantize_h(0, T)
+                sort_w1(ahead, slice(1, 2))
+            elif c < F_GROUPS - 1:
+                j = ahead - F_GROUPS
+                add_base(j, 0)
+                quantize_h(0, T)
+                add_base(j, 1)
+            else:
+                quantize_h(0, HALF_TOKENS)
+                quantize_h(HALF_TOKENS, T)
 
-        def vector_group(c):
-            vector_gain(c)
-            interleave_shared(c)
-            if c + AHEAD < FG:
-                sort_w1(c + AHEAD)
-            elif c < FG - 1:
-                first = RB_RATE * (c + AHEAD - FG)
-                for piece in pieces[first : first + RB_RATE + (RB_MORE if c == FG - 2 else 0)]:
-                    residual_bias(*piece)
-            quantize_h(c)
-
-        resident = pieces[:RES]
-        narrow = 8 - RES
-        slots = (FG - LAG) * PACK
-        home = dict(zip(resident, [4, 5, 6, 7, 3, 2]))
-        for k, piece in enumerate(pieces[RES:]):
-            home[piece] = (slots + k) % narrow
-        for c in range(FG):
-            wide = c < LAG
-            down = [(c - LAG, j, h) for j, h in resident] if not wide else []
-            if c == 0:
-                accs = [bank(t) for t in range(PACK)]
-                for t in range(G0):
-                    up_pass(accs[t], c, t, 0)
+        cuts = [(len(resident) * t + PACK // 2) // PACK for t in range(PACK + 1)]
+        opened = [bank(t) for t in range(WIDE_RING)]
+        for t in range(2):
+            up_pass(opened[t], 0, t, 0)
+        for c in range(F_GROUPS):
             for t in range(PACK):
                 if c == 0:
-                    acc = accs[t]
-                    for g in range(1 if t < G0 else 0, DG):
-                        up_pass(acc, c, t, g)
+                    acc = opened[t]
                 else:
-                    acc = bank(t if wide else ((c - LAG) * PACK + t) % narrow)
-                    for g in range(DG):
-                        up_pass(acc, c, t, g)
-                gelu_out(c, t, acc)
+                    acc = bank(t % (WIDE_RING if c < DOWN_LAG else NARROW_RING))
+                for g in range(1 if c == 0 and t < 2 else 0, D_GROUPS):
+                    up_pass(acc, c, t, g)
+                apply_gelu(c, t, acc)
                 if t > 0:
-                    scalar_gain(c, t - 1)
+                    gain_on_scalar(c, t - 1)
                 elif c > 0:
-                    scalar_gain(c - 1, PACK - 1)
-                    vector_group(c - 1)
-                for item in down[(RES * t + 2) // PACK : (RES * (t + 1) + 2) // PACK]:
+                    gain_on_scalar(c - 1, PACK - 1)
+                    finish_h(c - 1)
+                if c >= DOWN_LAG:
+                    for j, h in resident[cuts[t] : cuts[t + 1]]:
+                        down_pass(c - DOWN_LAG, j, h)
+        gain_on_scalar(F_GROUPS - 1, PACK - 1)
+        finish_h(F_GROUPS - 1)
+
+        late = [(c, j, h) for j, h in late_pieces for c in range(F_GROUPS)]
+        for c in range(F_GROUPS - DOWN_LAG, F_GROUPS):
+            if c == F_GROUPS - 1:
+                for item in late[:LATE_BEFORE_LAST_GROUP]:
                     down_pass(*item)
-        scalar_gain(FG - 1, PACK - 1)
-        vector_group(FG - 1)
-
-        late = [(c, j, h) for j, h in pieces[RES:] for c in range(FG)]
-        marks = [0] * (LAG - 1) + [EARLY_A, EARLY_B]
-        for k in range(LAG):
-            for item in late[marks[k] : marks[k + 1]]:
-                down_pass(*item)
             for j, h in resident:
-                down_pass(FG - LAG + k, j, h)
-        late = late[EARLY_B:]
+                down_pass(c, j, h)
+        late = late[LATE_BEFORE_LAST_GROUP:]
 
-        y_codes = [kept("y_codes%d" % pair, [P, DG, 2 * P], U32) for pair in range(TT // 2)]
-        y_scales = kept("y_scales", [P, DG, T], U8)
+        y = [kept("y%d" % j, [P, D], F32) for j in range(TOKEN_TILES)]
+        y_codes = [kept("y_codes%d" % half, [P, D_GROUPS, HALF_TOKENS], U32) for half in range(2)]
+        y_scales = kept("y_scales", [P, D_GROUPS, T], U8)
         words_out = out_1.rearrange("g p m t -> p g (m t)").bitcast(I32)
-        y = [kept("y%d" % j, [P, D], F32) for j in range(TT)]
+        last = TOKEN_TILES - 1
         y_pairs = {}
-        y_t = {}
+        y_turned = {}
         y_grouped = {}
 
-        def add_residual(j, h):
-            if (j, h) not in rb:
-                residual_bias(j, h)
-            cols = slice(h * KP, (h + 1) * KP)
-            nc.vector.tensor_tensor(out=y[j][:, cols], in0=y_acc[j, h][:], in1=rb[j, h][:], op=ALU.add)
-            if j == TT - 1:
+        def add_y(j, h):
+            cols = slice(h * GROUP, (h + 1) * GROUP)
+            nc.vector.tensor_tensor(out=y[j][:, cols], in0=y_acc[j, h][:], in1=base[j, h][:], op=ALU.add)
+            if j == last:
                 nc.sync.dma_start(out=out_0[j * P : (j + 1) * P, cols], in_=y[j][:, cols])
-            elif h == DG - 1:
+            elif h == D_GROUPS - 1:
                 nc.sync.dma_start(out=out_0[j * P : (j + 1) * P, :], in_=y[j][:])
 
-        def by_pairs(ap):
-            return ap.rearrange("p (m u e) -> p u m e", u=2, e=2)
+        def by_pairs(values):
+            return values.rearrange("p (m u e) -> p u m e", u=2, e=2)
 
-        def round_y(j, h, direct):
-            y_pairs[j, h] = kept("y_pairs%d_%d" % (j, h), [P, KP], BF16)
-            dst = y_pairs[j, h][:].rearrange("p (u m e) -> p u m e", u=2, e=2)
-            if direct:
-                nc.vector.tensor_tensor(out=dst, in0=by_pairs(y_acc[j, h][:]), in1=by_pairs(rb[j, h][:]), op=ALU.add)
-            else:
-                nc.scalar.copy(out=dst, in_=by_pairs(y[j][:, h * KP : (h + 1) * KP]))
+        def new_pairs(j, h):
+            y_pairs[j, h] = kept("y_pairs%d_%d" % (j, h), [P, GROUP], BF16)
+            return y_pairs[j, h][:].rearrange("p (u m e) -> p u m e", u=2, e=2)
 
-        def turn_y(j, halves, index):
-            y_t[j, halves] = bank(index)
+        def round_y(j, h):
+            nc.scalar.copy(out=new_pairs(j, h), in_=by_pairs(y[j][:, h * GROUP : (h + 1) * GROUP]))
+
+        def turn_y(j, groups, index):
+            y_turned[j, groups] = bank(index)
             for u in range(2):
-                for k, h in enumerate(halves):
+                for k, h in enumerate(groups):
                     words = y_pairs[j, h][:].bitcast(F32)
-                    col = (len(halves) * u + k) * P
-                    nc.tensor.transpose(y_t[j, halves][:, col : col + P], words[:, u * P : (u + 1) * P], ident[:])
+                    col = (len(groups) * u + k) * P
+                    nc.tensor.transpose(
+                        y_turned[j, groups][:, col : col + P], words[:, u * P : (u + 1) * P], ident[:]
+                    )
 
-        def group_y(j, halves):
-            n = len(halves)
-            y_grouped[j, halves] = kept("y_grouped%d_%d" % (j, halves[0]), [P, n * KP], BF16)
+        def group_y(j, groups):
+            n = len(groups)
+            y_grouped[j, groups] = kept("y_grouped%d_%d" % (j, groups[0]), [P, n * GROUP], BF16)
             nc.scalar.copy(
-                out=y_grouped[j, halves][:].bitcast(F32).rearrange("p (r u) -> p r u", u=2),
-                in_=y_t[j, halves][:, 0 : 2 * n * P].rearrange("p (u r) -> p r u", u=2),
+                out=y_grouped[j, groups][:].bitcast(F32).rearrange("p (m u) -> p m u", u=2),
+                in_=y_turned[j, groups][:, 0 : 2 * n * P].rearrange("p (u m) -> p m u", u=2),
             )
 
-        def quantize_y(j, halves):
-            for k, h in enumerate(halves):
+        def quantize_y(j, groups):
+            for k, h in enumerate(groups):
                 nc.vector.quantize_mx(
                     out=y_codes[j // 2][:, h, (j % 2) * P : (j % 2 + 1) * P].bitcast(FP8X4),
                     scales=y_scales[:, h, j * P : (j + 1) * P],
-                    in_=y_grouped[j, halves][:, k * KP : (k + 1) * KP],
+                    in_=y_grouped[j, groups][:, k * GROUP : (k + 1) * GROUP],
                 )
-            if j % 2 == 1 and halves[-1] == DG - 1:
+            if j % 2 == 1 and groups[-1] == D_GROUPS - 1:
                 nc.sync.dma_start(out=words_out[:, :, (j - 1) * P : (j + 1) * P], in_=y_codes[j // 2][:].bitcast(I32))
 
-        both = (0, 1)
-        last = TT - 1
+        both = tuple(range(D_GROUPS))
         for j, h in resident[:4]:
-            add_residual(j, h)
-            round_y(j, h, False)
-        for item in late[:STEP]:
+            add_y(j, h)
+            round_y(j, h)
+        for item in late[:LATE_BEFORE_TURNS]:
             down_pass(*item)
-        turn_y(0, both, 4)
-        turn_y(1, both, 5)
-        for item in late[STEP:]:
+        turn_y(0, both, RESIDENT_BANKS[0])
+        turn_y(1, both, RESIDENT_BANKS[1])
+        for item in late[LATE_BEFORE_TURNS:]:
             down_pass(*item)
         for j, h in resident[4:]:
-            add_residual(j, h)
-            round_y(j, h, False)
+            add_y(j, h)
+            round_y(j, h)
         group_y(0, both)
-        add_residual(last, 0)
-        round_y(last, 0, False)
+        add_base(last, 0)
+        add_y(last, 0)
         group_y(1, both)
-        residual_bias(last, 1)
+        round_y(last, 0)
+        add_base(last, 1)
         quantize_y(0, both)
-        turn_y(2, both, 6)
-        turn_y(last, (0,), 7)
-        round_y(last, 1, True)
-        add_residual(last, 1)
-        turn_y(last, (1,), 3)
-        group_y(2, both)
         quantize_y(1, both)
+        turn_y(2, both, RESIDENT_BANKS[2])
+        turn_y(last, (0,), RESIDENT_BANKS[3])
+        nc.vector.tensor_tensor(
+            out=new_pairs(last, 1), in0=by_pairs(y_acc[last, 1][:]), in1=by_pairs(base[last, 1][:]), op=ALU.add
+        )
+        add_y(last, 1)
+        turn_y(last, (1,), RESIDENT_BANKS[4])
+        group_y(2, both)
         group_y(last, (0,))
         group_y(last, (1,))
         quantize_y(2, both)
         quantize_y(last, (0,))
         quantize_y(last, (1,))
-        for q in range(4):
-            queue = nc.sync if q % 2 == 0 else nc.scalar
+        for r in range(SCALE_ROWS):
+            queue = nc.sync if r % 2 == 0 else nc.scalar
             queue.dma_start(
-                out=out_2[:, q:16:4, :].rearrange("g r n -> r g n").bitcast(I32),
-                in_=y_scales[q:P:32, :, :].bitcast(I32),
+                out=out_2[:, r:BLOCKS:SCALE_ROWS, :].rearrange("g q n -> q g n").bitcast(I32),
+                in_=y_scales[r:P:QUAD, :, :].bitcast(I32),
             )

@@ -25,14 +25,14 @@ BLOCKS = GROUP // 32
 D_GROUPS = D // GROUP
 F_GROUPS = F // GROUP
 TOKEN_TILES = T // P
-ALIGN = 64
+ALIGN = 256
 RUN = 4
 
 DOWN_LAG = 3
 SORT_AHEAD = 4
 
-SHARE_FROM = 2
 SCALAR_TOKENS = 304
+SCALAR_TOKENS_FIRST = 128
 HALF_TOKENS = T // 2
 
 WIDE_RING = 4
@@ -104,7 +104,6 @@ def tile_gelu_feedforward_residual_head_h1_kernel(
         nc.scalar.dma_start(
             out=vector_rows[F_GROUPS : 2 * F_GROUPS, :], in_=mid_scale.rearrange("(c n) -> c n", n=GROUP)
         )
-        load_w1(1)
 
         w1_dense_sorted = kept("w1_dense_sorted", [P, dense_cols], U8)
         nc.vector.tensor_copy(
@@ -119,7 +118,7 @@ def tile_gelu_feedforward_residual_head_h1_kernel(
                     out=w1_planes[g][r:P:QUAD, :, :].rearrange("p c n -> p (c n)").bitcast(I32),
                     in_=w1_dense_sorted[first : first + per_group, :].bitcast(I32),
                 )
-        for c in range(2, SORT_AHEAD + 1):
+        for c in range(1, SORT_AHEAD + 1):
             load_w1(c)
         for r in range(SCALE_ROWS):
             nc.sync.dma_start(
@@ -222,7 +221,9 @@ def tile_gelu_feedforward_residual_head_h1_kernel(
         def scalar_tokens(c):
             if c == F_GROUPS - 1:
                 return HALF_TOKENS
-            return SCALAR_TOKENS if c >= SHARE_FROM else 0
+            if c == DOWN_LAG - 1:
+                return SCALAR_TOKENS_FIRST
+            return SCALAR_TOKENS if c >= DOWN_LAG else 0
 
         def apply_gelu(c, t, acc):
             if t == 0:

from contextlib import ExitStack

import concourse.mybir as mybir
from concourse.masks import make_identity

T, D, F = 512, 1024, 4096
FLOPS = 2 * 2 * T * D * F

F32 = mybir.dt.float32
BF16 = mybir.dt.bfloat16
I32 = mybir.dt.int32
U32 = mybir.dt.uint32
U8 = mybir.dt.uint8
FP8X4 = mybir.dt.float8_e4m3fn_x4
FP4X4 = mybir.dt.float4_e2m1fn_x4
ALU = mybir.AluOpType
ACT = mybir.ActivationFunctionType

P = 128
PACK = 4
GROUP = P * PACK
QUAD = 32
SCALE_ROWS = 4
BLOCKS = GROUP // 32
D_GROUPS = D // GROUP
F_GROUPS = F // GROUP
TOKEN_TILES = T // P
ALIGN = 256
RUN = 4

DOWN_LAG = 3
SORT_AHEAD = 4

SCALAR_TOKENS = 304
SCALAR_TOKENS_FIRST = 128
HALF_TOKENS = T // 2

WIDE_RING = 4
NARROW_RING = 2
X_BANKS = 4
VECTOR_BANK = 3
RESIDENT_BANKS = [4, 5, 6, 7, 3, 2]
LATE_BEFORE_LAST_GROUP = 3
LATE_BEFORE_TURNS = 6


def tile_gelu_feedforward_residual_head_h1_kernel(
    tc, states, in_scale, w1_words, w1_scales, b1, mid_scale, w2_words, w2_scales, b2, out_0, out_1, out_2
):
    nc = tc.nc
    with ExitStack() as ctx:
        keep = ctx.enter_context(tc.tile_pool(name="keep", bufs=1))
        work = ctx.enter_context(tc.tile_pool(name="work", bufs=2))
        psum = ctx.enter_context(tc.psum_pool(name="psum", bufs=1))
        ctx.enter_context(tc.manual_schedule())

        def kept(name, shape, dtype):
            return keep.tile(shape, dtype, name=name, tag=name, align_bytes=ALIGN)

        def bank(index):
            return psum.tile([P, GROUP], F32, name="bank%d" % index, tag="bank%d" % index)

        ident = kept("ident", [P, P], F32)
        make_identity(nc, ident[:])
        vector_rows = kept("vector_rows", [P, GROUP], BF16)
        nc.vector.memset(vector_rows[:].bitcast(I32), 0)
        w1_planes = [kept("w1_plane%d" % g, [P, F_GROUPS, GROUP], U8) for g in range(D_GROUPS)]
        w2_plane = kept("w2_plane", [P, F_GROUPS, D], U8)
        for plane in w1_planes + [w2_plane]:
            nc.vector.memset(plane[:].rearrange("p c n -> p (c n)").bitcast(I32), 0)

        dense_cols = D_GROUPS * BLOCKS * F // P
        w1_dense = kept("w1_dense", [P, dense_cols], U8)
        by_row = w1_scales.rearrange("g (q r) n -> r (g q) n", r=SCALE_ROWS)
        for r in range(SCALE_ROWS):
            nc.sync.dma_start(out=w1_dense[QUAD * r : QUAD * (r + 1), :].bitcast(I32), in_=by_row[r].bitcast(I32))
        x_gain = kept("x_gain", [P, D_GROUPS, PACK], BF16)
        nc.scalar.dma_start(out=x_gain[:], in_=in_scale.rearrange("(g p t) -> p g t", p=P, t=PACK))

        w1_raw = []

        def load_w1(c):
            raw = kept("w1_raw%d" % c, [P, D_GROUPS, 2 * GROUP], U8)
            src = w1_words[:, :, 2 * GROUP * c : 2 * GROUP * (c + 1)].rearrange("g p n -> p g n")
            nc.sync.dma_start(out=raw[:].bitcast(I32), in_=src.bitcast(I32))
            w1_raw.append(raw)

        w2 = []

        def load_w2(pair):
            words = kept("w2_%d" % pair, [P, 2, 2 * D], U8)
            src = w2_words[2 * pair : 2 * pair + 2].rearrange("g p n -> p g n")
            nc.sync.dma_start(out=words[:].bitcast(I32), in_=src.bitcast(I32))
            w2.append(words)

        load_w1(0)
        rows = {}
        for g in range(D_GROUPS):
            for half in range(2):
                rows[g, half] = kept("rows%d_%d" % (g, half), [P, 2, GROUP], BF16)
                src = states[half * HALF_TOKENS : (half + 1) * HALF_TOKENS, g * GROUP : (g + 1) * GROUP]
                nc.sync.dma_start(out=rows[g, half][:], in_=src.rearrange("(j p) n -> p j n", p=P))
        nc.scalar.dma_start(out=vector_rows[0:F_GROUPS, :], in_=b1.rearrange("(c n) -> c n", n=GROUP))
        nc.scalar.dma_start(
            out=vector_rows[F_GROUPS : 2 * F_GROUPS, :], in_=mid_scale.rearrange("(c n) -> c n", n=GROUP)
        )

        w1_dense_sorted = kept("w1_dense_sorted", [P, dense_cols], U8)
        nc.vector.tensor_copy(
            out=w1_dense_sorted[:].rearrange("p (c t m) -> p c t m", t=PACK, m=P),
            in_=w1_dense[:].rearrange("p (c m t) -> p c t m", t=PACK, m=P),
        )
        per_group = QUAD // D_GROUPS
        for g in range(D_GROUPS):
            for r in range(SCALE_ROWS):
                first = QUAD * r + per_group * g
                nc.sync.dma_start(
                    out=w1_planes[g][r:P:QUAD, :, :].rearrange("p c n -> p (c n)").bitcast(I32),
                    in_=w1_dense_sorted[first : first + per_group, :].bitcast(I32),
                )
        for c in range(1, SORT_AHEAD + 1):
            load_w1(c)
        for r in range(SCALE_ROWS):
            nc.sync.dma_start(
                out=w2_plane[r:P:QUAD, :, :].bitcast(I32),
                in_=w2_scales[:, r:BLOCKS:SCALE_ROWS, :].rearrange("c q n -> q c n").bitcast(I32),
            )
        load_w2(0)
        for c in range(SORT_AHEAD + 1, F_GROUPS):
            load_w1(c)
            load_w2(c - SORT_AHEAD)
        b2_rows = kept("b2_rows", [P, D], BF16)
        nc.sync.dma_start(out=b2_rows[:], in_=b2.partition_broadcast(P))

        w1 = [kept("w1_%d" % c, [P, D_GROUPS, PACK, 2 * P], U8) for c in range(F_GROUPS)]

        def sort_w1(c, groups):
            nc.vector.tensor_copy(
                out=w1[c][:, groups].rearrange("p g t (m b) -> p g t m b", b=2),
                in_=w1_raw[c][:, groups].rearrange("p g (m t b) -> p g t m b", t=PACK, b=2),
            )

        def turn_words(src, acc, col, stride):
            words = src.bitcast(F32)
            for u in range(2):
                nc.tensor.transpose(acc[:, col + u * stride : col + u * stride + P], words[:, u::2], ident[:])

        x_grouped = [kept("x_grouped%d" % g, [P, T * PACK], BF16) for g in range(D_GROUPS)]
        x_codes = [kept("x_codes%d" % g, [P, T], U32) for g in range(D_GROUPS)]
        x_scales = [kept("x_scales%d" % g, [P, T], U8) for g in range(D_GROUPS)]

        def scale_x(g, half):
            acc = bank(X_BANKS + 2 * g + half)
            for tile in range(2):
                turn_words(rows[g, half][:, tile, :], acc, tile * P, HALF_TOKENS)
            cols = slice(half * HALF_TOKENS * PACK, (half + 1) * HALF_TOKENS * PACK)
            gain = x_gain[:, g : g + 1, :].rearrange("p o (u e) -> p o u e", e=2)
            nc.vector.tensor_tensor(
                out=x_grouped[g][:, cols].rearrange("p (m u e) -> p m u e", u=2, e=2),
                in0=acc[:].bitcast(BF16).rearrange("p (u m e) -> p m u e", u=2, e=2),
                in1=gain.to_broadcast([P, HALF_TOKENS, 2, 2]),
                op=ALU.mult,
            )

        def quantize_x(g):
            nc.vector.quantize_mx(out=x_codes[g][:].bitcast(FP8X4), scales=x_scales[g][:], in_=x_grouped[g][:])

        all_groups = slice(0, D_GROUPS)
        sort_w1(0, all_groups)
        scale_x(0, 0)
        scale_x(0, 1)
        scale_x(1, 0)
        quantize_x(0)
        scale_x(1, 1)
        channel = kept("channel", [P, 2 * F_GROUPS, PACK], F32)
        turned = bank(VECTOR_BANK)
        turn_words(vector_rows[:], turned, 0, P)
        turned_values = turned[:, 0 : 2 * P].bitcast(BF16).rearrange("p (u c e) -> p c u e", u=2, e=2)
        nc.vector.tensor_copy(
            out=channel[:].rearrange("p c (u e) -> p c u e", e=2), in_=turned_values[:, 0 : 2 * F_GROUPS]
        )
        quantize_x(1)
        for c in range(1, SORT_AHEAD):
            sort_w1(c, all_groups)

        pieces = [(j, h) for j in range(TOKEN_TILES) for h in range(D_GROUPS)]
        resident = pieces[: len(RESIDENT_BANKS)]
        late_pieces = pieces[len(RESIDENT_BANKS) :]
        home = dict(zip(pieces, RESIDENT_BANKS + list(range(NARROW_RING))))
        h_codes = [kept("h_codes%d" % c, [P, T], U32) for c in range(F_GROUPS)]
        h_scales = [kept("h_scales%d" % c, [P, T], U8) for c in range(F_GROUPS)]
        gelu = {}
        scalar_part = {}
        y_acc = {}
        base = {}

        def up_pass(acc, c, t, g):
            nc.tensor.matmul_mx(
                out=acc[:],
                lhsT=w1[c][:, g, t, :].bitcast(FP4X4),
                lhsT_scale=w1_planes[g][:, c, t * P : (t + 1) * P],
                rhs=x_codes[g][:].bitcast(FP8X4),
                rhs_scale=x_scales[g][:],
                start=(g == 0),
                stop=(g == D_GROUPS - 1),
            )

        def down_pass(c, j, h):
            if c == 0:
                y_acc[j, h] = bank(home[j, h])
            nc.tensor.matmul_mx(
                out=y_acc[j, h][:],
                lhsT=h_codes[c][:, j * P : (j + 1) * P].bitcast(FP8X4),
                lhsT_scale=h_scales[c][:, j * P : (j + 1) * P],
                rhs=w2[c // 2][:, c % 2, 2 * GROUP * h : 2 * GROUP * (h + 1)].bitcast(FP4X4),
                rhs_scale=w2_plane[:, c, GROUP * h : GROUP * (h + 1)],
                start=(c == 0),
                stop=(c == F_GROUPS - 1),
            )

        def scalar_tokens(c):
            if c == F_GROUPS - 1:
                return HALF_TOKENS
            if c == DOWN_LAG - 1:
                return SCALAR_TOKENS_FIRST
            return SCALAR_TOKENS if c >= DOWN_LAG else 0

        def apply_gelu(c, t, acc):
            if t == 0:
                gelu[c] = work.tile(
                    [P, PACK, T], F32, name="gelu", tag="gelu", bufs=DOWN_LAG + 1, align_bytes=ALIGN
                )
            nc.scalar.activation(
                out=gelu[c][:, t, :], in_=acc[:], func=ACT.Gelu_apprx_tanh, bias=channel[:, c, t : t + 1]
            )

        def gain_on_scalar(c, t):
            n = scalar_tokens(c)
            if n == 0:
                return
            if t == 0:
                scalar_part[c] = work.tile(
                    [P, PACK, n], BF16, name="scalar_part", tag="scalar_part", align_bytes=ALIGN
                )
            nc.scalar.activation(
                out=scalar_part[c][:, t, :],
                in_=gelu[c][:, t, T - n : T],
                func=ACT.Copy,
                scale=channel[:, F_GROUPS + c, t : t + 1],
            )

        def add_base(j, h):
            base[j, h] = kept("base%d_%d" % (j, h), [P, GROUP], F32)
            nc.vector.tensor_tensor(
                out=base[j, h][:],
                in0=rows[h, j // 2][:, j % 2, :],
                in1=b2_rows[:, h * GROUP : (h + 1) * GROUP],
                op=ALU.add,
            )

        def finish_h(c):
            n = scalar_tokens(c)
            grouped = work.tile([P, T, PACK], BF16, name="h_grouped", tag="h_grouped", align_bytes=ALIGN)
            gain = channel[:, F_GROUPS + c : F_GROUPS + c + 1, :].unsqueeze(3)
            nc.vector.tensor_tensor(
                out=grouped[:, 0 : T - n, :].rearrange("p (a i) t -> p a t i", i=RUN),
                in0=gelu[c][:, :, 0 : T - n].rearrange("p t (a i) -> p a t i", i=RUN),
                in1=gain.to_broadcast([P, (T - n) // RUN, PACK, RUN]),
                op=ALU.mult,
            )
            if n > 0:
                nc.vector.tensor_copy(
                    out=grouped[:, T - n : T, :].rearrange("p (a i) t -> p a t i", i=RUN),
                    in_=scalar_part[c][:].rearrange("p t (a i) -> p a t i", i=RUN),
                )

            def quantize_h(lo, hi):
                nc.vector.quantize_mx(
                    out=h_codes[c][:, lo:hi].bitcast(FP8X4),
                    scales=h_scales[c][:, lo:hi],
                    in_=grouped[:, lo:hi, :].rearrange("p m t -> p (m t)"),
                )

            ahead = c + SORT_AHEAD
            if ahead < F_GROUPS:
                sort_w1(ahead, slice(0, 1))
                quantize_h(0, T)
                sort_w1(ahead, slice(1, 2))
            elif c < F_GROUPS - 1:
                j = ahead - F_GROUPS
                add_base(j, 0)
                quantize_h(0, T)
                add_base(j, 1)
            else:
                quantize_h(0, HALF_TOKENS)
                quantize_h(HALF_TOKENS, T)

        cuts = [(len(resident) * t + PACK // 2) // PACK for t in range(PACK + 1)]
        opened = [bank(t) for t in range(WIDE_RING)]
        for t in range(2):
            up_pass(opened[t], 0, t, 0)
        for c in range(F_GROUPS):
            for t in range(PACK):
                if c == 0:
                    acc = opened[t]
                else:
                    acc = bank(t % (WIDE_RING if c < DOWN_LAG else NARROW_RING))
                for g in range(1 if c == 0 and t < 2 else 0, D_GROUPS):
                    up_pass(acc, c, t, g)
                apply_gelu(c, t, acc)
                if t > 0:
                    gain_on_scalar(c, t - 1)
                elif c > 0:
                    gain_on_scalar(c - 1, PACK - 1)
                    finish_h(c - 1)
                if c >= DOWN_LAG:
                    for j, h in resident[cuts[t] : cuts[t + 1]]:
                        down_pass(c - DOWN_LAG, j, h)
        gain_on_scalar(F_GROUPS - 1, PACK - 1)
        finish_h(F_GROUPS - 1)

        late = [(c, j, h) for j, h in late_pieces for c in range(F_GROUPS)]
        for c in range(F_GROUPS - DOWN_LAG, F_GROUPS):
            if c == F_GROUPS - 1:
                for item in late[:LATE_BEFORE_LAST_GROUP]:
                    down_pass(*item)
            for j, h in resident:
                down_pass(c, j, h)
        late = late[LATE_BEFORE_LAST_GROUP:]

        y = [kept("y%d" % j, [P, D], F32) for j in range(TOKEN_TILES)]
        y_codes = [kept("y_codes%d" % half, [P, D_GROUPS, HALF_TOKENS], U32) for half in range(2)]
        y_scales = kept("y_scales", [P, D_GROUPS, T], U8)
        words_out = out_1.rearrange("g p m t -> p g (m t)").bitcast(I32)
        last = TOKEN_TILES - 1
        y_pairs = {}
        y_turned = {}
        y_grouped = {}

        def add_y(j, h):
            cols = slice(h * GROUP, (h + 1) * GROUP)
            nc.vector.tensor_tensor(out=y[j][:, cols], in0=y_acc[j, h][:], in1=base[j, h][:], op=ALU.add)
            if j == last:
                nc.sync.dma_start(out=out_0[j * P : (j + 1) * P, cols], in_=y[j][:, cols])
            elif h == D_GROUPS - 1:
                nc.sync.dma_start(out=out_0[j * P : (j + 1) * P, :], in_=y[j][:])

        def by_pairs(values):
            return values.rearrange("p (m u e) -> p u m e", u=2, e=2)

        def new_pairs(j, h):
            y_pairs[j, h] = kept("y_pairs%d_%d" % (j, h), [P, GROUP], BF16)
            return y_pairs[j, h][:].rearrange("p (u m e) -> p u m e", u=2, e=2)

        def round_y(j, h):
            nc.scalar.copy(out=new_pairs(j, h), in_=by_pairs(y[j][:, h * GROUP : (h + 1) * GROUP]))

        def turn_y(j, groups, index):
            y_turned[j, groups] = bank(index)
            for u in range(2):
                for k, h in enumerate(groups):
                    words = y_pairs[j, h][:].bitcast(F32)
                    col = (len(groups) * u + k) * P
                    nc.tensor.transpose(
                        y_turned[j, groups][:, col : col + P], words[:, u * P : (u + 1) * P], ident[:]
                    )

        def group_y(j, groups):
            n = len(groups)
            y_grouped[j, groups] = kept("y_grouped%d_%d" % (j, groups[0]), [P, n * GROUP], BF16)
            nc.scalar.copy(
                out=y_grouped[j, groups][:].bitcast(F32).rearrange("p (m u) -> p m u", u=2),
                in_=y_turned[j, groups][:, 0 : 2 * n * P].rearrange("p (u m) -> p m u", u=2),
            )

        def quantize_y(j, groups):
            for k, h in enumerate(groups):
                nc.vector.quantize_mx(
                    out=y_codes[j // 2][:, h, (j % 2) * P : (j % 2 + 1) * P].bitcast(FP8X4),
                    scales=y_scales[:, h, j * P : (j + 1) * P],
                    in_=y_grouped[j, groups][:, k * GROUP : (k + 1) * GROUP],
                )
            if j % 2 == 1 and groups[-1] == D_GROUPS - 1:
                nc.sync.dma_start(out=words_out[:, :, (j - 1) * P : (j + 1) * P], in_=y_codes[j // 2][:].bitcast(I32))

        both = tuple(range(D_GROUPS))
        for j, h in resident[:4]:
            add_y(j, h)
            round_y(j, h)
        for item in late[:LATE_BEFORE_TURNS]:
            down_pass(*item)
        turn_y(0, both, RESIDENT_BANKS[0])
        turn_y(1, both, RESIDENT_BANKS[1])
        for item in late[LATE_BEFORE_TURNS:]:
            down_pass(*item)
        for j, h in resident[4:]:
            add_y(j, h)
            round_y(j, h)
        group_y(0, both)
        add_base(last, 0)
        add_y(last, 0)
        group_y(1, both)
        round_y(last, 0)
        add_base(last, 1)
        quantize_y(0, both)
        quantize_y(1, both)
        turn_y(2, both, RESIDENT_BANKS[2])
        turn_y(last, (0,), RESIDENT_BANKS[3])
        nc.vector.tensor_tensor(
            out=new_pairs(last, 1), in0=by_pairs(y_acc[last, 1][:]), in1=by_pairs(base[last, 1][:]), op=ALU.add
        )
        add_y(last, 1)
        turn_y(last, (1,), RESIDENT_BANKS[4])
        group_y(2, both)
        group_y(last, (0,))
        group_y(last, (1,))
        quantize_y(2, both)
        quantize_y(last, (0,))
        quantize_y(last, (1,))
        for r in range(SCALE_ROWS):
            queue = nc.sync if r % 2 == 0 else nc.scalar
            queue.dma_start(
                out=out_2[:, r:BLOCKS:SCALE_ROWS, :].rearrange("g q n -> q g n").bitcast(I32),
                in_=y_scales[r:P:QUAD, :, :].bitcast(I32),
            )
